import numpy as np
import ml_dtypes


def mxq(x, axis, fmt="e4m3"):
    dtype, down = {"e4m3": (ml_dtypes.float8_e4m3fn, 7), "e5m2": (ml_dtypes.float8_e5m2, 14)}[fmt]
    v = np.moveaxis(np.asarray(x, np.float32).astype(ml_dtypes.bfloat16).astype(np.float64), axis, -1)
    blocks = v.reshape(v.shape[:-1] + (-1, 32))
    amax = np.abs(blocks).max(-1, keepdims=True)
    byte = np.maximum(np.where(amax > 0, np.frexp(amax)[1] - 1 + 127, 0) - down, 1)
    scale = np.exp2(byte - 127.0)
    codes = (blocks / scale).astype(np.float32).astype(dtype).astype(np.float64)
    return np.moveaxis((codes * scale).reshape(v.shape), -1, axis)


WIDE = False


def mx_kscale(k):
    if not WIDE:
        return np.ones(k)
    levels = np.array([10, -10, 5, -5, 0])
    if k % 512:
        return np.exp2(np.random.permutation(np.resize(levels, k // 32))).repeat(32)
    a = np.empty((k // 512, 16))
    for p in range(k // 512):
        a[p, :8] = np.random.permutation(np.resize(levels, 8))
        for g in range(8):
            far = levels[np.abs(levels - a[p, g]) >= 10]
            a[p, g + 8] = far[np.random.randint(len(far))]
    return np.exp2(a.ravel()).repeat(32)


def f64(x):
    return np.asarray(x).astype(np.float64)


def striped(idx):
    return np.tile(idx.reshape(-1, 16).T, (8, 1)).astype(np.uint16)


def unstriped(offs):
    return offs[:16].T.reshape(-1).astype(np.int64)


E2M1 = np.array([0.0, 0.5, 1.0, 1.5, 2.0, 3.0, 4.0, 6.0, -0.0, -0.5, -1.0, -1.5, -2.0, -3.0, -4.0, -6.0])


def pack_weight(w, fmt):
    k, n = w.shape
    w = f64(np.asarray(w, np.float32).astype(ml_dtypes.bfloat16)).reshape(k // 32, 32, n)
    amax = np.abs(w).max(1)
    if fmt == "e4m3":
        byte = np.frexp(amax)[1] - 1 + 127 - 7
    else:
        mant, ex = np.frexp(amax / 6.0)
        byte = np.where(mant > 0.5, ex, ex - 1) + 127
    byte = np.clip(np.where(amax > 0, byte, 1), 1, 254)
    scaled = (w * np.exp2(127.0 - byte)[:, None, :]).reshape(k, n).astype(np.float32)
    by_word = np.ascontiguousarray(scaled.reshape(k // 512, 128, 4, n).transpose(0, 1, 3, 2))
    if fmt == "e4m3":
        words = by_word.astype(ml_dtypes.float8_e4m3fn).view(np.uint8)
    else:
        c = by_word.astype(ml_dtypes.float4_e2m1fn).view(np.uint8) & 0xF
        words = (c[..., 0::2] | (c[..., 1::2] << 4)).reshape(k // 512, 128, 2 * n)
    return np.ascontiguousarray(words), np.ascontiguousarray(byte.astype(np.uint8).reshape(k // 512, 16, n))


def unpack_weight(words, scales, fmt):
    g, _, n = scales.shape
    words = np.ascontiguousarray(words).reshape(g, 128, n, -1)
    if fmt == "e4m3":
        vals = words.view(ml_dtypes.float8_e4m3fn).astype(np.float64)
    else:
        nib = np.empty((g, 128, n, 4), np.uint8)
        nib[..., 0::2] = words & 0xF
        nib[..., 1::2] = words >> 4
        vals = E2M1[nib]
    vals = vals * np.repeat(np.exp2(scales.astype(np.float64) - 127.0), 8, axis=1)[..., None]
    return vals.transpose(0, 1, 3, 2).reshape(g * 512, n)


def gelu(v):
    return 0.5 * v * (1.0 + np.tanh(np.sqrt(2.0 / np.pi) * (v + 0.044715 * v**3)))


K, T, S, H, T2, S2 = 1024, 2048, 512, 1024, 4096, 1024

def setup_inputs():
    n = np.random.standard_normal
    s = mx_kscale(K)[:, None]
    u = mx_kscale(H)[:, None]
    tab_words, tab_scales = pack_weight(n((K, T)) * s, "e4m3")
    tab2_words, tab2_scales = pack_weight(n((H, T2)) / np.sqrt(H) / u, "e4m3")
    w4_words, w4_scales = pack_weight(n((K, H)) / np.sqrt(K) / s, "e2m1")
    return {
        "tab_words": tab_words, "tab_scales": tab_scales,
        "offs": striped(np.random.permutation(T)[:S]),
        "tab2_words": tab2_words, "tab2_scales": tab2_scales,
        "offs2": striped(np.random.permutation(T2)[:S2]),
        "w1": (n((K, H)) / np.sqrt(K) / s * u.T).astype(np.float32),
        "b1": (0.5 * n(H) * u[:, 0]).astype(np.float32),
        "w4_words": w4_words, "w4_scales": w4_scales,
        "bc": (0.5 * n(S2)).astype(np.float32),
    }

def reference(tab_words, tab_scales, offs, tab2_words, tab2_scales, offs2, w1, b1, w4_words, w4_scales, bc):
    v = unpack_weight(tab_words, tab_scales, "e4m3")[:, unstriped(offs)]
    v2 = unpack_weight(tab2_words, tab2_scales, "e4m3")[:, unstriped(offs2)]
    w4 = unpack_weight(w4_words, w4_scales, "e2m1")
    a = (mxq(f64(w1), 0, "e4m3").T @ v) + f64(b1)[:, None]
    b = w4.T @ v
    h = a * b
    y = v2.T @ mxq(h, 0, "e4m3")
    return y + f64(bc)[:, None]

@@ -1,0 +1,309 @@
+from contextlib import ExitStack
+
+import concourse.mybir as mybir
+from concourse.masks import make_identity
+
+K, T, S, H, T2, S2 = 1024, 2048, 512, 1024, 4096, 1024
+FLOPS = 2 * (2 * K * H * S + H * S2 * S)
+
+F32 = mybir.dt.float32
+BF16 = mybir.dt.bfloat16
+I32 = mybir.dt.int32
+U32 = mybir.dt.uint32
+U16 = mybir.dt.uint16
+U8 = mybir.dt.uint8
+FP8X4 = mybir.dt.float8_e4m3fn_x4
+FP4X4 = mybir.dt.float4_e2m1fn_x4
+IDENTITY = mybir.ActivationFunctionType.Identity
+MULT = mybir.AluOpType.mult
+ADD = mybir.AluOpType.add
+
+P = 128
+PACK = 4
+PASS = P * PACK
+PASSES = 2
+HALF = S // 2
+
+
+def tile_list_ad_bid_scores_kernel(
+    tc, tab_words, tab_scales, offs, tab2_words, tab2_scales, offs2, w1, b1, w4_words, w4_scales, bc, out
+):
+    nc = tc.nc
+    with ExitStack() as ctx:
+        lists = ctx.enter_context(tc.tile_pool(name="lists", bufs=1))
+        keep = ctx.enter_context(tc.tile_pool(name="keep", bufs=1))
+        psum = ctx.enter_context(tc.psum_pool(name="psum", bufs=1))
+
+        def held(name, shape, dtype):
+            return keep.tile(shape, dtype, name=name, align_bytes=64)
+
+        def bank(index, shape):
+            return psum.tile(shape, F32, name="bank%d" % index, tag="bank%d" % index)
+
+        idx = lists.tile([P, S // 16], U16, name="idx")
+        idx2 = lists.tile([P, S2 // 16], U16, name="idx2")
+
+        tab_plane = held("tab_plane", [P, PASSES, T // 4], I32)
+        w4_plane = held("w4_plane", [P, PASSES, H // 4], I32)
+        tab2_plane = held("tab2_plane", [P, T2 // 4], I32)
+        bc_rows = held("bc_rows", [P, P], F32)
+        w4_raw = held("w4_raw", [P, PASSES, H // 2], I32)
+        b1_col = held("b1_col", [P, PASSES, PACK], F32)
+        w1_raw = {(b, a): held("w1_raw%d%d" % (b, a), [P, PACK, PASS], F32) for b in range(2) for a in range(2)}
+        tab_win = [held("tab_win%d" % a, [P, T], I32) for a in range(2)]
+        tab2_win = [held("tab2_win%d" % a, [P, T2], I32) for a in range(2)]
+        v_scale = held("v_scale", [P, PASSES, S], U8)
+        w4_scale = held("w4_scale", [P, PASSES, H], U8)
+        v2_scale = held("v2_scale", [P, S2], U8)
+        w1_codes = held("w1_codes", [P, PASSES, PASSES, PASS], U32)
+        w1_scale = held("w1_scale", [P, PASSES, PASSES, PASS], U8)
+        w4_codes = held("w4_codes", [P, PASSES, 2 * H], U8)
+        v_codes = held("v_codes", [P, PASSES, S], U32)
+        v2_codes = held("v2_codes", [P, PASSES, S2], U32)
+        h_codes = held("h_codes", [P, PASSES, S], U32)
+        h_scale = held("h_scale", [P, PASSES, S], U8)
+        a_sb = [held("a_sb%d" % b, [P, PACK, S], F32) for b in range(2)]
+        h_bf = [held("h_bf%d" % b, [P, S * PACK], BF16) for b in range(2)]
+        ident = held("ident", [P, P], F32)
+        bc_col = held("bc_col", [P, S2 // P], F32)
+        w1_bf = {}
+        a_bank = {}
+        b_bank = {}
+        y_bank = {}
+
+        def load_plane(plane, scales):
+            for r in range(4):
+                nc.sync.dma_start(
+                    out=plane[r:P:32, :, :], in_=scales.bitcast(I32)[:, r:16:4, :].rearrange("a q n -> q a n")
+                )
+
+        def load_tab2_plane():
+            for q in range(4):
+                nc.sync.dma_start(
+                    out=tab2_plane[32 * q + 4 : 32 * q + 12, :],
+                    in_=tab2_scales.bitcast(I32)[:, 4 * q : 4 * q + 4, :],
+                )
+
+        def load_w1(b, a):
+            rows = w1[a * PASS : (a + 1) * PASS, b * PASS : (b + 1) * PASS]
+            nc.sync.dma_start(out=w1_raw[b, a][:], in_=rows.rearrange("(p j) c -> p j c", j=PACK))
+
+        def load_words(win, words):
+            nc.sync.dma_start(out=win[:], in_=words.rearrange("p t i -> p (t i)").bitcast(I32))
+
+        def load_w4():
+            nc.sync.dma_start(out=w4_raw[:], in_=w4_words.bitcast(I32).rearrange("a p n -> p a n"))
+
+        def load_biases():
+            nc.sync.dma_start(out=b1_col[:], in_=b1.rearrange("(b p t) -> p b t", b=PASSES, t=PACK))
+            nc.sync.dma_start(out=bc_rows[0 : S2 // P, :], in_=bc.rearrange("(c p) -> c p", p=P))
+
+        def turn_bc():
+            make_identity(nc, ident[:])
+            bc_bank = bank(7, [P, P])
+            nc.tensor.transpose(bc_bank[:], bc_rows[:], ident[:])
+            nc.scalar.copy(out=bc_col[:], in_=bc_bank[:, 0 : S2 // P])
+
+        def permute_w4_codes():
+            nc.vector.tensor_copy(
+                out=w4_codes[:].bitcast(U16).rearrange("p a (b t m) -> p (a b) t m", b=PASSES, t=PACK),
+                in_=w4_raw[:].bitcast(U16).rearrange("p a (b m t) -> p (a b) t m", b=PASSES, t=PACK),
+            )
+
+        def permute_w4_scale():
+            nc.vector.tensor_copy(
+                out=w4_scale[:].rearrange("p a (b t m) -> p (a b) t m", b=PASSES, t=PACK),
+                in_=w4_plane[:].bitcast(U8).rearrange("p a (b m t) -> p (a b) t m", b=PASSES, t=PACK),
+            )
+
+        def gather_v_scale(a):
+            nc.vector.tensor_copy(v_scale[:, a, :], tab_plane[:, a, :].bitcast(U8).indirect(idx[:]))
+
+        def gather_v(a):
+            nc.vector.tensor_copy(v_codes[:, a, :], tab_win[a][:].bitcast(U32).indirect(idx[:]))
+
+        def gather_v2_scale():
+            nc.vector.tensor_copy(v2_scale[:], tab2_plane[:].bitcast(U8).indirect(idx2[:]))
+
+        def gather_v2(b, half):
+            n = S2 // 2
+            nc.vector.tensor_copy(
+                v2_codes[:, b, half * n : (half + 1) * n],
+                tab2_win[b][:].bitcast(U32).indirect(idx2[:, half * n // 16 : (half + 1) * n // 16]),
+            )
+
+        def round_w1(b, a, u, copy):
+            w1_bf[b, a, u] = held("w1_bf%d%d%d" % (b, a, u), [P, PASS * 2], BF16)
+            copy(
+                out=w1_bf[b, a, u][:].rearrange("p (t m j) -> p m j t", t=2, j=PACK),
+                in_=w1_raw[b, a][:].rearrange("p j (m t) -> p m j t", t=PACK)[:, :, :, 2 * u : 2 * u + 2],
+            )
+
+        def quantise_w1(b, a, u):
+            cols = slice(2 * u * P, 2 * (u + 1) * P)
+            nc.vector.quantize_mx(
+                out=w1_codes[:, b, a, cols].bitcast(FP8X4), scales=w1_scale[:, b, a, cols], in_=w1_bf[b, a, u][:]
+            )
+
+        def project_a(b, a):
+            for t in range(PACK):
+                if a == 0:
+                    a_bank[b, t] = bank(t, [P, S])
+                cols = slice(t * P, (t + 1) * P)
+                nc.tensor.matmul_mx(
+                    out=a_bank[b, t][:],
+                    lhsT=w1_codes[:, b, a, cols].bitcast(FP8X4),
+                    lhsT_scale=w1_scale[:, b, a, cols],
+                    rhs=v_codes[:, a, :].bitcast(FP8X4),
+                    rhs_scale=v_scale[:, a, :],
+                    start=(a == 0),
+                    stop=(a == PASSES - 1),
+                )
+
+        def add_b1(b, width):
+            for j in range(0, S, width):
+                for t in range(PACK):
+                    nc.scalar.activation(
+                        out=a_sb[b][:, t, j : j + width],
+                        in_=a_bank[b, t][:, j : j + width],
+                        func=IDENTITY,
+                        bias=b1_col[:, b, t : t + 1],
+                    )
+
+        def project_b(b):
+            for c in range(S // P):
+                b_bank[b, c] = bank(PACK + c, [P, PACK, P])
+                js = slice(c * P, (c + 1) * P)
+                for t in range(PACK):
+                    col = b * PASS + t * P
+                    for a in range(PASSES):
+                        nc.tensor.matmul_mx(
+                            out=b_bank[b, c][:, t, :],
+                            lhsT=w4_codes[:, a, 2 * col : 2 * (col + P)].bitcast(FP4X4),
+                            lhsT_scale=w4_scale[:, a, col : col + P],
+                            rhs=v_codes[:, a, js].bitcast(FP8X4),
+                            rhs_scale=v_scale[:, a, js],
+                            start=(a == 0),
+                            stop=(a == PASSES - 1),
+                        )
+
+        def interact(b, c):
+            nc.vector.tensor_tensor(
+                out=h_bf[b][:, c * PASS : (c + 1) * PASS].rearrange("p (g i t) -> p g t i", i=4, t=PACK),
+                in0=b_bank[b, c][:].rearrange("p t (g i) -> p g t i", i=4),
+                in1=a_sb[b][:, :, c * P : (c + 1) * P].rearrange("p t (g i) -> p g t i", i=4),
+                op=MULT,
+            )
+
+        def quantise_h(b, half):
+            js = slice(half * HALF, (half + 1) * HALF)
+            nc.vector.quantize_mx(
+                out=h_codes[:, b, js].bitcast(FP8X4),
+                scales=h_scale[:, b, js],
+                in_=h_bf[b][:, half * 2 * S : (half + 1) * 2 * S],
+            )
+
+        def score(b, half):
+            for c in range(4 * half, 4 * half + 4):
+                if b == 0:
+                    y_bank[c] = bank(c, [P, S])
+                cols = slice(c * P, (c + 1) * P)
+                nc.tensor.matmul_mx(
+                    out=y_bank[c][:],
+                    lhsT=v2_codes[:, b, cols].bitcast(FP8X4),
+                    lhsT_scale=v2_scale[4 * (b + 1) : P, cols],
+                    rhs=h_codes[:, b, :].bitcast(FP8X4),
+                    rhs_scale=h_scale[:, b, :],
+                    start=(b == 0),
+                    stop=(b == PASSES - 1),
+                )
+
+        def store(c, on_vector):
+            y_sb = held("y_sb%d" % c, [P, S], F32)
+            if on_vector:
+                nc.vector.tensor_scalar(
+                    out=y_sb[:], in0=y_bank[c][:], scalar1=bc_col[:, c : c + 1], scalar2=None, op0=ADD
+                )
+            else:
+                nc.scalar.activation(out=y_sb[:], in_=y_bank[c][:], func=IDENTITY, bias=bc_col[:, c : c + 1])
+            nc.sync.dma_start(out=out[c * P : (c + 1) * P, :], in_=y_sb[:])
+
+        nc.vector.memset(w4_plane[:], 0)
+        nc.vector.memset(tab_plane[:], 0)
+        nc.vector.memset(bc_rows[:], 0.0)
+        nc.vector.memset(tab2_plane[:], 0)
+        nc.sync.dma_start(idx[:], offs)
+        load_w4()
+        load_plane(tab_plane, tab_scales)
+        load_biases()
+        load_words(tab_win[0], tab_words[0])
+        load_plane(w4_plane, w4_scales)
+        load_words(tab_win[1], tab_words[1])
+        nc.sync.dma_start(idx2[:], offs2)
+        load_tab2_plane()
+        load_w1(0, 0)
+        load_w1(0, 1)
+        load_w1(1, 1)
+        load_w1(1, 0)
+        load_words(tab2_win[0], tab2_words[0])
+        load_words(tab2_win[1], tab2_words[1])
+        turn_bc()
+        round_w1(1, 1, 0, nc.vector.tensor_copy)
+        gather_v2(0, 1)
+        quantise_w1(1, 1, 0)
+        gather_v(1)
+        round_w1(0, 0, 1, nc.scalar.copy)
+        round_w1(0, 1, 0, nc.scalar.copy)
+        permute_w4_codes()
+        gather_v2(1, 0)
+        quantise_w1(0, 0, 1)
+        gather_v_scale(1)
+        quantise_w1(0, 1, 0)
+        round_w1(1, 0, 0, nc.scalar.copy)
+        quantise_w1(1, 0, 0)
+        round_w1(0, 0, 0, nc.scalar.copy)
+        quantise_w1(0, 0, 0)
+        round_w1(0, 1, 1, nc.vector.tensor_copy)
+        quantise_w1(0, 1, 1)
+        gather_v2(0, 0)
+        gather_v_scale(0)
+        gather_v(0)
+        project_a(0, 0)
+        project_a(0, 1)
+        add_b1(0, 256)
+        permute_w4_scale()
+        project_b(0)
+        interact(0, 0)
+        interact(0, 2)
+        interact(0, 3)
+        quantise_h(0, 1)
+        round_w1(1, 1, 1, nc.vector.tensor_copy)
+        quantise_w1(1, 1, 1)
+        interact(0, 1)
+        quantise_h(0, 0)
+        project_b(1)
+        round_w1(1, 0, 1, nc.scalar.copy)
+        quantise_w1(1, 0, 1)
+        project_a(1, 0)
+        project_a(1, 1)
+        add_b1(1, 256)
+        interact(1, 0)
+        interact(1, 1)
+        quantise_h(1, 0)
+        interact(1, 2)
+        interact(1, 3)
+        quantise_h(1, 1)
+        gather_v2_scale()
+        score(0, 1)
+        gather_v2(1, 1)
+        score(1, 1)
+        store(5, False)
+        store(4, True)
+        store(6, True)
+        store(7, True)
+        score(0, 0)
+        score(1, 0)
+        store(0, False)
+        store(2, False)
+        store(1, True)
+        store(3, True)

@@ -51,7 +51,7 @@ def tile_list_ad_bid_scores_kernel(
         b1_col = held("b1_col", [P, PASSES, PACK], F32)
         w1_raw = {(b, a): held("w1_raw%d%d" % (b, a), [P, PACK, PASS], F32) for b in range(2) for a in range(2)}
         tab_win = [held("tab_win%d" % a, [P, T], I32) for a in range(2)]
-        tab2_win = [held("tab2_win%d" % a, [P, T2], I32) for a in range(2)]
+        tab2_win = [keep.tile([P, T2], I32, name="tab2_win%d" % a, tag="tab2_win%d" % a, align_bytes=64) for a in range(2)]
         v_scale = held("v_scale", [P, PASSES, S], U8)
         w4_scale = held("w4_scale", [P, PASSES, H], U8)
         v2_scale = held("v2_scale", [P, S2], U8)
@@ -59,7 +59,7 @@ def tile_list_ad_bid_scores_kernel(
         w1_scale = held("w1_scale", [P, PASSES, PASSES, PASS], U8)
         w4_codes = held("w4_codes", [P, PASSES, 2 * H], U8)
         v_codes = held("v_codes", [P, PASSES, S], U32)
-        v2_codes = held("v2_codes", [P, PASSES, S2], U32)
+        v2_codes = {}
         h_codes = held("h_codes", [P, PASSES, S], U32)
         h_scale = held("h_scale", [P, PASSES, S], U8)
         a_sb = [held("a_sb%d" % b, [P, PACK, S], F32) for b in range(2)]
@@ -79,7 +79,7 @@ def tile_list_ad_bid_scores_kernel(
 
         def load_tab2_plane():
             for q in range(4):
-                nc.sync.dma_start(
+                nc.gpsimd.dma_start(
                     out=tab2_plane[32 * q + 4 : 32 * q + 12, :],
                     in_=tab2_scales.bitcast(I32)[:, 4 * q : 4 * q + 4, :],
                 )
@@ -127,8 +127,11 @@ def tile_list_ad_bid_scores_kernel(
 
         def gather_v2(b, half):
             n = S2 // 2
+            name = "v2_codes%d%d" % (b, half)
+            tag = "tab2_win1" if (b, half) == (0, 1) else name
+            v2_codes[b, half] = keep.tile([P, n], U32, name=name, tag=tag, align_bytes=64)
             nc.vector.tensor_copy(
-                v2_codes[:, b, half * n : (half + 1) * n],
+                v2_codes[b, half][:],
                 tab2_win[b][:].bitcast(U32).indirect(idx2[:, half * n // 16 : (half + 1) * n // 16]),
             )
 
@@ -203,19 +206,20 @@ def tile_list_ad_bid_scores_kernel(
                 in_=h_bf[b][:, half * 2 * S : (half + 1) * 2 * S],
             )
 
-        def score(b, half):
+        def score(step, half):
+            b = step if half == 0 else 1 - step
             for c in range(4 * half, 4 * half + 4):
-                if b == 0:
-                    y_bank[c] = bank(c, [P, S])
+                if step == 0:
+                    y_bank[c] = bank((c + 4) % 8, [P, S])
                 cols = slice(c * P, (c + 1) * P)
                 nc.tensor.matmul_mx(
                     out=y_bank[c][:],
-                    lhsT=v2_codes[:, b, cols].bitcast(FP8X4),
+                    lhsT=v2_codes[b, half][:, (c % 4) * P : (c % 4 + 1) * P].bitcast(FP8X4),
                     lhsT_scale=v2_scale[4 * (b + 1) : P, cols],
                     rhs=h_codes[:, b, :].bitcast(FP8X4),
                     rhs_scale=h_scale[:, b, :],
-                    start=(b == 0),
-                    stop=(b == PASSES - 1),
+                    start=(step == 0),
+                    stop=(step == PASSES - 1),
                 )
 
         def store(c, on_vector):
@@ -230,80 +234,80 @@ def tile_list_ad_bid_scores_kernel(
 
         nc.vector.memset(w4_plane[:], 0)
         nc.vector.memset(tab_plane[:], 0)
-        nc.vector.memset(bc_rows[:], 0.0)
-        nc.vector.memset(tab2_plane[:], 0)
-        nc.sync.dma_start(idx[:], offs)
-        load_w4()
-        load_plane(tab_plane, tab_scales)
-        load_biases()
-        load_words(tab_win[0], tab_words[0])
-        load_plane(w4_plane, w4_scales)
-        load_words(tab_win[1], tab_words[1])
-        nc.sync.dma_start(idx2[:], offs2)
+        nc.gpsimd.memset(tab2_plane[:], 0)
         load_tab2_plane()
+        nc.gpsimd.memset(bc_rows[:], 0.0)
+        load_w4()
+        load_plane(w4_plane, w4_scales)
+        load_plane(tab_plane, tab_scales)
+        nc.sync.dma_start(idx[:], offs)
+        load_words(tab_win[0], tab_words[0])
+        load_words(tab_win[1], tab_words[1])
+        load_biases()
+        nc.sync.dma_start(idx2[:], offs2)
         load_w1(0, 0)
         load_w1(0, 1)
-        load_w1(1, 1)
         load_w1(1, 0)
+        load_w1(1, 1)
         load_words(tab2_win[0], tab2_words[0])
         load_words(tab2_win[1], tab2_words[1])
         turn_bc()
-        round_w1(1, 1, 0, nc.vector.tensor_copy)
-        gather_v2(0, 1)
-        quantise_w1(1, 1, 0)
-        gather_v(1)
-        round_w1(0, 0, 1, nc.scalar.copy)
-        round_w1(0, 1, 0, nc.scalar.copy)
         permute_w4_codes()
-        gather_v2(1, 0)
-        quantise_w1(0, 0, 1)
+        permute_w4_scale()
+        gather_v_scale(0)
         gather_v_scale(1)
-        quantise_w1(0, 1, 0)
-        round_w1(1, 0, 0, nc.scalar.copy)
-        quantise_w1(1, 0, 0)
+        gather_v(0)
+        gather_v(1)
+        round_w1(0, 0, 1, nc.vector.tensor_copy)
         round_w1(0, 0, 0, nc.scalar.copy)
+        quantise_w1(0, 0, 1)
         quantise_w1(0, 0, 0)
         round_w1(0, 1, 1, nc.vector.tensor_copy)
+        round_w1(0, 1, 0, nc.scalar.copy)
         quantise_w1(0, 1, 1)
-        gather_v2(0, 0)
-        gather_v_scale(0)
-        gather_v(0)
+        quantise_w1(0, 1, 0)
         project_a(0, 0)
+        project_b(0)
         project_a(0, 1)
         add_b1(0, 256)
-        permute_w4_scale()
-        project_b(0)
+        round_w1(1, 0, 1, nc.vector.tensor_copy)
+        round_w1(1, 0, 0, nc.scalar.copy)
+        round_w1(1, 1, 1, nc.vector.tensor_copy)
+        round_w1(1, 1, 0, nc.scalar.copy)
+        quantise_w1(1, 0, 1)
+        quantise_w1(1, 0, 0)
+        quantise_w1(1, 1, 1)
+        quantise_w1(1, 1, 0)
         interact(0, 0)
+        interact(0, 1)
         interact(0, 2)
         interact(0, 3)
-        quantise_h(0, 1)
-        round_w1(1, 1, 1, nc.vector.tensor_copy)
-        quantise_w1(1, 1, 1)
-        interact(0, 1)
-        quantise_h(0, 0)
-        project_b(1)
-        round_w1(1, 0, 1, nc.scalar.copy)
-        quantise_w1(1, 0, 1)
         project_a(1, 0)
         project_a(1, 1)
+        quantise_h(0, 0)
+        quantise_h(0, 1)
         add_b1(1, 256)
+        project_b(1)
         interact(1, 0)
         interact(1, 1)
-        quantise_h(1, 0)
         interact(1, 2)
+        quantise_h(1, 0)
         interact(1, 3)
         quantise_h(1, 1)
         gather_v2_scale()
-        score(0, 1)
-        gather_v2(1, 1)
-        score(1, 1)
-        store(5, False)
-        store(4, True)
-        store(6, True)
-        store(7, True)
+        gather_v2(1, 0)
+        gather_v2(0, 0)
         score(0, 0)
         score(1, 0)
+        gather_v2(1, 1)
+        gather_v2(0, 1)
+        score(0, 1)
+        score(1, 1)
         store(0, False)
+        store(1, False)
         store(2, False)
-        store(1, True)
-        store(3, True)
+        store(3, False)
+        store(4, False)
+        store(5, True)
+        store(6, False)
+        store(7, True)

@@ -34,8 +34,8 @@ def tile_list_ad_bid_scores_kernel(
         keep = ctx.enter_context(tc.tile_pool(name="keep", bufs=1))
         psum = ctx.enter_context(tc.psum_pool(name="psum", bufs=1))
 
-        def held(name, shape, dtype):
-            return keep.tile(shape, dtype, name=name, align_bytes=64)
+        def held(name, shape, dtype, tag=None):
+            return keep.tile(shape, dtype, name=name, tag=tag or name, align_bytes=64)
 
         def bank(index, shape):
             return psum.tile(shape, F32, name="bank%d" % index, tag="bank%d" % index)
@@ -43,7 +43,7 @@ def tile_list_ad_bid_scores_kernel(
         idx = lists.tile([P, S // 16], U16, name="idx")
         idx2 = lists.tile([P, S2 // 16], U16, name="idx2")
 
-        tab_plane = held("tab_plane", [P, PASSES, T // 4], I32)
+        tab_planes = held("tab_planes", [P, PASSES, T // 4], I32)
         w4_plane = held("w4_plane", [P, PASSES, H // 4], I32)
         tab2_plane = held("tab2_plane", [P, T2 // 4], I32)
         bc_rows = held("bc_rows", [P, P], F32)
@@ -51,21 +51,21 @@ def tile_list_ad_bid_scores_kernel(
         b1_col = held("b1_col", [P, PASSES, PACK], F32)
         w1_raw = {(b, a): held("w1_raw%d%d" % (b, a), [P, PACK, PASS], F32) for b in range(2) for a in range(2)}
         tab_win = [held("tab_win%d" % a, [P, T], I32) for a in range(2)]
-        tab2_win = [keep.tile([P, T2], I32, name="tab2_win%d" % a, tag="tab2_win%d" % a, align_bytes=64) for a in range(2)]
-        v_scale = held("v_scale", [P, PASSES, S], U8)
+        tab2_win = [held("tab2_win%d" % a, [P, T2], I32) for a in range(2)]
+        v_scale = [held("v_scale%d" % a, [P, S], U8) for a in range(2)]
         w4_scale = held("w4_scale", [P, PASSES, H], U8)
-        v2_scale = held("v2_scale", [P, S2], U8)
-        w1_codes = held("w1_codes", [P, PASSES, PASSES, PASS], U32)
-        w1_scale = held("w1_scale", [P, PASSES, PASSES, PASS], U8)
+        w1_codes = {}
+        w1_scale = {(b, a): held("w1_scale%d%d" % (b, a), [P, PASS], U8) for b in range(2) for a in range(2)}
         w4_codes = held("w4_codes", [P, PASSES, 2 * H], U8)
-        v_codes = held("v_codes", [P, PASSES, S], U32)
-        v2_codes = {}
-        h_codes = held("h_codes", [P, PASSES, S], U32)
-        h_scale = held("h_scale", [P, PASSES, S], U8)
-        a_sb = [held("a_sb%d" % b, [P, PACK, S], F32) for b in range(2)]
-        h_bf = [held("h_bf%d" % b, [P, S * PACK], BF16) for b in range(2)]
+        h_codes = {}
+        h_scale = [held("h_scale%d" % b, [P, S], U8) for b in range(2)]
+        a_sb = {(b, h): held("a_sb%d%d" % (b, h), [P, PACK, HALF], F32) for b in range(2) for h in range(2)}
+        h_bf = {}
         ident = held("ident", [P, P], F32)
         bc_col = held("bc_col", [P, S2 // P], F32)
+        v_codes = {}
+        v2_codes = {}
+        v2_scale = {}
         w1_bf = {}
         a_bank = {}
         b_bank = {}
@@ -78,7 +78,7 @@ def tile_list_ad_bid_scores_kernel(
                 )
 
         def load_tab2_plane():
-            for q in range(4):
+            for q in (0, 2, 1, 3):
                 nc.gpsimd.dma_start(
                     out=tab2_plane[32 * q + 4 : 32 * q + 12, :],
                     in_=tab2_scales.bitcast(I32)[:, 4 * q : 4 * q + 4, :],
@@ -95,11 +95,10 @@ def tile_list_ad_bid_scores_kernel(
             nc.sync.dma_start(out=w4_raw[:], in_=w4_words.bitcast(I32).rearrange("a p n -> p a n"))
 
         def load_biases():
-            nc.sync.dma_start(out=b1_col[:], in_=b1.rearrange("(b p t) -> p b t", b=PASSES, t=PACK))
-            nc.sync.dma_start(out=bc_rows[0 : S2 // P, :], in_=bc.rearrange("(c p) -> c p", p=P))
+            nc.gpsimd.dma_start(out=b1_col[:], in_=b1.rearrange("(b p t) -> p b t", b=PASSES, t=PACK))
+            nc.gpsimd.dma_start(out=bc_rows[0 : S2 // P, :], in_=bc.rearrange("(c p) -> c p", p=P))
 
         def turn_bc():
-            make_identity(nc, ident[:])
             bc_bank = bank(7, [P, P])
             nc.tensor.transpose(bc_bank[:], bc_rows[:], ident[:])
             nc.scalar.copy(out=bc_col[:], in_=bc_bank[:, 0 : S2 // P])
@@ -117,19 +116,31 @@ def tile_list_ad_bid_scores_kernel(
             )
 
         def gather_v_scale(a):
-            nc.vector.tensor_copy(v_scale[:, a, :], tab_plane[:, a, :].bitcast(U8).indirect(idx[:]))
+            nc.vector.tensor_copy(v_scale[a][:], tab_planes[:, a, :].bitcast(U8).indirect(idx[:]))
 
-        def gather_v(a):
-            nc.vector.tensor_copy(v_codes[:, a, :], tab_win[a][:].bitcast(U32).indirect(idx[:]))
+        def gather_v(a, first, n):
+            codes = held("v_codes%d_%d" % (a, first), [P, n], U32)
+            nc.vector.tensor_copy(
+                codes[:], tab_win[a][:].bitcast(U32).indirect(idx[:, first // 16 : (first + n) // 16])
+            )
+            for c in range(first // P, (first + n) // P):
+                v_codes[a, c] = (codes, c * P - first)
 
-        def gather_v2_scale():
-            nc.vector.tensor_copy(v2_scale[:], tab2_plane[:].bitcast(U8).indirect(idx2[:]))
+        def v_cols(a, first, n):
+            codes, at = v_codes[a, first // P]
+            return codes[:, at : at + n].bitcast(FP8X4)
+
+        def gather_v2_scale(half, tag):
+            n = S2 // 2
+            v2_scale[half] = held("v2_scale%d" % half, [P, n], U8, tag)
+            nc.vector.tensor_copy(
+                v2_scale[half][:],
+                tab2_plane[:].bitcast(U8).indirect(idx2[:, half * n // 16 : (half + 1) * n // 16]),
+            )
 
         def gather_v2(b, half):
             n = S2 // 2
-            name = "v2_codes%d%d" % (b, half)
-            tag = "tab2_win1" if (b, half) == (0, 1) else name
-            v2_codes[b, half] = keep.tile([P, n], U32, name=name, tag=tag, align_bytes=64)
+            v2_codes[b, half] = held("v2_codes%d%d" % (b, half), [P, n], U32, "tab2_win1" if (b, half) == (0, 1) else None)
             nc.vector.tensor_copy(
                 v2_codes[b, half][:],
                 tab2_win[b][:].bitcast(U32).indirect(idx2[:, half * n // 16 : (half + 1) * n // 16]),
@@ -143,81 +154,84 @@ def tile_list_ad_bid_scores_kernel(
             )
 
         def quantise_w1(b, a, u):
+            if (b, a) not in w1_codes:
+                w1_codes[b, a] = held("w1_codes%d%d" % (b, a), [P, PASS], U32)
             cols = slice(2 * u * P, 2 * (u + 1) * P)
             nc.vector.quantize_mx(
-                out=w1_codes[:, b, a, cols].bitcast(FP8X4), scales=w1_scale[:, b, a, cols], in_=w1_bf[b, a, u][:]
+                out=w1_codes[b, a][:, cols].bitcast(FP8X4), scales=w1_scale[b, a][:, cols], in_=w1_bf[b, a, u][:]
             )
 
-        def project_a(b, a):
-            for t in range(PACK):
+        def project_a(b, a, h):
+            js = slice(h * HALF, (h + 1) * HALF)
+            for u in range(2):
                 if a == 0:
-                    a_bank[b, t] = bank(t, [P, S])
-                cols = slice(t * P, (t + 1) * P)
-                nc.tensor.matmul_mx(
-                    out=a_bank[b, t][:],
-                    lhsT=w1_codes[:, b, a, cols].bitcast(FP8X4),
-                    lhsT_scale=w1_scale[:, b, a, cols],
-                    rhs=v_codes[:, a, :].bitcast(FP8X4),
-                    rhs_scale=v_scale[:, a, :],
-                    start=(a == 0),
-                    stop=(a == PASSES - 1),
-                )
-
-        def add_b1(b, width):
-            for j in range(0, S, width):
-                for t in range(PACK):
-                    nc.scalar.activation(
-                        out=a_sb[b][:, t, j : j + width],
-                        in_=a_bank[b, t][:, j : j + width],
-                        func=IDENTITY,
-                        bias=b1_col[:, b, t : t + 1],
+                    a_bank[b, h, u] = bank(2 * h + u, [P, 2, HALF])
+                for e in range(2):
+                    cols = slice((2 * u + e) * P, (2 * u + e + 1) * P)
+                    nc.tensor.matmul_mx(
+                        out=a_bank[b, h, u][:, e, :],
+                        lhsT=w1_codes[b, a][:, cols].bitcast(FP8X4),
+                        lhsT_scale=w1_scale[b, a][:, cols],
+                        rhs=v_cols(a, h * HALF, HALF),
+                        rhs_scale=v_scale[a][:, js],
+                        start=(a == 0 and e == 0),
+                        stop=(a == PASSES - 1 and e == 1),
                     )
 
-        def project_b(b):
-            for c in range(S // P):
+        def add_b1(b, h):
+            for t in range(PACK):
+                nc.scalar.activation(
+                    out=a_sb[b, h][:, t, :],
+                    in_=a_bank[b, h, t // 2][:, t % 2, :],
+                    func=IDENTITY,
+                    bias=b1_col[:, b, t : t + 1],
+                )
+
+        def project_b(b, a, c):
+            if a == 0:
                 b_bank[b, c] = bank(PACK + c, [P, PACK, P])
-                js = slice(c * P, (c + 1) * P)
-                for t in range(PACK):
-                    col = b * PASS + t * P
-                    for a in range(PASSES):
-                        nc.tensor.matmul_mx(
-                            out=b_bank[b, c][:, t, :],
-                            lhsT=w4_codes[:, a, 2 * col : 2 * (col + P)].bitcast(FP4X4),
-                            lhsT_scale=w4_scale[:, a, col : col + P],
-                            rhs=v_codes[:, a, js].bitcast(FP8X4),
-                            rhs_scale=v_scale[:, a, js],
-                            start=(a == 0),
-                            stop=(a == PASSES - 1),
-                        )
+            js = slice(c * P, (c + 1) * P)
+            for t in range(PACK):
+                col = b * PASS + t * P
+                nc.tensor.matmul_mx(
+                    out=b_bank[b, c][:, t, :],
+                    lhsT=w4_codes[:, a, 2 * col : 2 * (col + P)].bitcast(FP4X4),
+                    lhsT_scale=w4_scale[:, a, col : col + P],
+                    rhs=v_cols(a, c * P, P),
+                    rhs_scale=v_scale[a][:, js],
+                    start=(a == 0 and t == 0),
+                    stop=(a == PASSES - 1 and t == PACK - 1),
+                )
 
         def interact(b, c):
+            h, at = c // 2, (c % 2) * P
+            if at == 0:
+                h_bf[b, h] = held("h_bf%d%d" % (b, h), [P, HALF * PACK], BF16, "w1_bf111" if (b, h) == (0, 1) else None)
             nc.vector.tensor_tensor(
-                out=h_bf[b][:, c * PASS : (c + 1) * PASS].rearrange("p (g i t) -> p g t i", i=4, t=PACK),
+                out=h_bf[b, h][:, at * PACK : (at + P) * PACK].rearrange("p (g i t) -> p g t i", i=4, t=PACK),
                 in0=b_bank[b, c][:].rearrange("p t (g i) -> p g t i", i=4),
-                in1=a_sb[b][:, :, c * P : (c + 1) * P].rearrange("p t (g i) -> p g t i", i=4),
+                in1=a_sb[b, h][:, :, at : at + P].rearrange("p t (g i) -> p g t i", i=4),
                 op=MULT,
             )
 
-        def quantise_h(b, half):
-            js = slice(half * HALF, (half + 1) * HALF)
-            nc.vector.quantize_mx(
-                out=h_codes[:, b, js].bitcast(FP8X4),
-                scales=h_scale[:, b, js],
-                in_=h_bf[b][:, half * 2 * S : (half + 1) * 2 * S],
-            )
+        def quantise_h(b, h):
+            if h == 0:
+                h_codes[b] = held("h_codes%d" % b, [P, S], U32, None)
+            js = slice(h * HALF, (h + 1) * HALF)
+            nc.vector.quantize_mx(out=h_codes[b][:, js].bitcast(FP8X4), scales=h_scale[b][:, js], in_=h_bf[b, h][:])
 
         def score(step, half):
             b = step if half == 0 else 1 - step
             for c in range(4 * half, 4 * half + 4):
                 if step == 0:
-                    y_bank[c] = bank((c + 4) % 8, [P, S])
-                cols = slice(c * P, (c + 1) * P)
+                    y_bank[c] = bank(c, [P, S])
+                cols = slice((c % 4) * P, (c % 4 + 1) * P)
                 nc.tensor.matmul_mx(
                     out=y_bank[c][:],
-                    lhsT=v2_codes[b, half][:, (c % 4) * P : (c % 4 + 1) * P].bitcast(FP8X4),
-                    lhsT_scale=v2_scale[4 * (b + 1) : P, cols],
-                    rhs=h_codes[:, b, :].bitcast(FP8X4),
-                    rhs_scale=h_scale[:, b, :],
+                    lhsT=v2_codes[b, half][:, cols].bitcast(FP8X4),
+                    lhsT_scale=v2_scale[half][4 * (b + 1) : P, cols],
+                    rhs=h_codes[b][:].bitcast(FP8X4),
+                    rhs_scale=h_scale[b][:],
                     start=(step == 0),
                     stop=(step == PASSES - 1),
                 )
@@ -232,82 +246,90 @@ def tile_list_ad_bid_scores_kernel(
                 nc.scalar.activation(out=y_sb[:], in_=y_bank[c][:], func=IDENTITY, bias=bc_col[:, c : c + 1])
             nc.sync.dma_start(out=out[c * P : (c + 1) * P, :], in_=y_sb[:])
 
+        on_scalar, on_vector = nc.scalar.copy, nc.vector.tensor_copy
+
+        nc.vector.memset(tab_planes[:], 0)
+        nc.vector.memset(tab2_plane[:], 0)
         nc.vector.memset(w4_plane[:], 0)
-        nc.vector.memset(tab_plane[:], 0)
-        nc.gpsimd.memset(tab2_plane[:], 0)
+        nc.vector.memset(bc_rows[:], 0.0)
+        make_identity(nc, ident[:])
         load_tab2_plane()
-        nc.gpsimd.memset(bc_rows[:], 0.0)
-        load_w4()
-        load_plane(w4_plane, w4_scales)
-        load_plane(tab_plane, tab_scales)
-        nc.sync.dma_start(idx[:], offs)
-        load_words(tab_win[0], tab_words[0])
-        load_words(tab_win[1], tab_words[1])
         load_biases()
+        load_w4()
+        nc.sync.dma_start(idx[:], offs)
         nc.sync.dma_start(idx2[:], offs2)
+        load_plane(tab_planes, tab_scales)
         load_w1(0, 0)
+        load_words(tab_win[0], tab_words[0])
+        load_plane(w4_plane, w4_scales)
         load_w1(0, 1)
+        load_words(tab_win[1], tab_words[1])
         load_w1(1, 0)
         load_w1(1, 1)
         load_words(tab2_win[0], tab2_words[0])
         load_words(tab2_win[1], tab2_words[1])
-        turn_bc()
+
         permute_w4_codes()
-        permute_w4_scale()
         gather_v_scale(0)
         gather_v_scale(1)
-        gather_v(0)
-        gather_v(1)
-        round_w1(0, 0, 1, nc.vector.tensor_copy)
-        round_w1(0, 0, 0, nc.scalar.copy)
-        quantise_w1(0, 0, 1)
+        gather_v2_scale(0, "tab_planes")
+        round_w1(0, 0, 0, on_scalar)
+        round_w1(0, 0, 1, on_scalar)
+        gather_v(0, 0, S)
+        permute_w4_scale()
         quantise_w1(0, 0, 0)
-        round_w1(0, 1, 1, nc.vector.tensor_copy)
-        round_w1(0, 1, 0, nc.scalar.copy)
+        quantise_w1(0, 0, 1)
+        for h in range(2):
+            project_a(0, 0, h)
+        for c in range(4):
+            project_b(0, 0, c)
+        round_w1(0, 1, 0, on_scalar)
+        round_w1(0, 1, 1, on_vector)
         quantise_w1(0, 1, 1)
         quantise_w1(0, 1, 0)
-        project_a(0, 0)
-        project_b(0)
-        project_a(0, 1)
-        add_b1(0, 256)
-        round_w1(1, 0, 1, nc.vector.tensor_copy)
-        round_w1(1, 0, 0, nc.scalar.copy)
-        round_w1(1, 1, 1, nc.vector.tensor_copy)
-        round_w1(1, 1, 0, nc.scalar.copy)
-        quantise_w1(1, 0, 1)
-        quantise_w1(1, 0, 0)
-        quantise_w1(1, 1, 1)
-        quantise_w1(1, 1, 0)
+        for h in range(2):
+            gather_v(1, h * HALF, HALF)
+            project_a(0, 1, h)
+            project_b(0, 1, 2 * h)
+            project_b(0, 1, 2 * h + 1)
+        gather_v2_scale(1, "tab_win1")
+        add_b1(0, 0)
+        round_w1(1, 0, 0, on_scalar)
+        round_w1(1, 0, 1, on_scalar)
+        add_b1(0, 1)
         interact(0, 0)
         interact(0, 1)
+        quantise_h(0, 0)
+        round_w1(1, 1, 0, on_vector)
+        round_w1(1, 1, 1, on_vector)
+        quantise_w1(1, 0, 0)
+        quantise_w1(1, 1, 0)
+        quantise_w1(1, 0, 1)
+        quantise_w1(1, 1, 1)
         interact(0, 2)
         interact(0, 3)
-        project_a(1, 0)
-        project_a(1, 1)
-        quantise_h(0, 0)
         quantise_h(0, 1)
-        add_b1(1, 256)
-        project_b(1)
+        turn_bc()
+        for h in range(2):
+            project_a(1, 0, h)
+            project_a(1, 1, h)
+            add_b1(1, h)
+        for c in range(4):
+            project_b(1, 0, c)
+            project_b(1, 1, c)
         interact(1, 0)
         interact(1, 1)
         interact(1, 2)
         quantise_h(1, 0)
         interact(1, 3)
-        quantise_h(1, 1)
-        gather_v2_scale()
-        gather_v2(1, 0)
         gather_v2(0, 0)
+        quantise_h(1, 1)
         score(0, 0)
+        gather_v2(1, 0)
         score(1, 0)
         gather_v2(1, 1)
-        gather_v2(0, 1)
         score(0, 1)
+        gather_v2(0, 1)
         score(1, 1)
-        store(0, False)
-        store(1, False)
-        store(2, False)
-        store(3, False)
-        store(4, False)
-        store(5, True)
-        store(6, False)
-        store(7, True)
+        for c in range(8):
+            store(c, c in (5, 7))

@@ -272,7 +272,6 @@ def tile_list_ad_bid_scores_kernel(
         permute_w4_codes()
         gather_v_scale(0)
         gather_v_scale(1)
-        gather_v2_scale(0, "tab_planes")
         round_w1(0, 0, 0, on_scalar)
         round_w1(0, 0, 1, on_scalar)
         gather_v(0, 0, S)
@@ -292,7 +291,8 @@ def tile_list_ad_bid_scores_kernel(
             project_a(0, 1, h)
             project_b(0, 1, 2 * h)
             project_b(0, 1, 2 * h + 1)
-        gather_v2_scale(1, "tab_win1")
+        gather_v2_scale(0, "tab_win1")
+        gather_v2_scale(1, "tab_win0")
         add_b1(0, 0)
         round_w1(1, 0, 0, on_scalar)
         round_w1(1, 0, 1, on_scalar)

@@ -47,13 +47,16 @@ def tile_list_ad_bid_scores_kernel(
         w4_plane = held("w4_plane", [P, PASSES, H // 4], I32)
         tab2_plane = held("tab2_plane", [P, T2 // 4], I32)
         bc_rows = held("bc_rows", [P, P], F32)
+        b1_rows = held("b1_rows", [P, PASS], F32)
+        v2_plane = held("v2_plane", [P, S2 // 4], I32)
+        v2_picked = held("v2_picked", [P, S2], U8)
         w4_raw = held("w4_raw", [P, PASSES, H // 2], I32)
-        b1_col = held("b1_col", [P, PASSES, PACK], F32)
+        b1_col = held("b1_col", [P, PACK, PASSES], F32)
         w1_raw = {(b, a): held("w1_raw%d%d" % (b, a), [P, PACK, PASS], F32) for b in range(2) for a in range(2)}
         tab_win = [held("tab_win%d" % a, [P, T], I32) for a in range(2)]
         tab2_win = [held("tab2_win%d" % a, [P, T2], I32) for a in range(2)]
         v_scale = [held("v_scale%d" % a, [P, S], U8) for a in range(2)]
-        w4_scale = held("w4_scale", [P, PASSES, H], U8)
+        w4_scale = held("w4_scale", [P, PASSES, H], U8, "tab_win0")
         w1_codes = {}
         w1_scale = {(b, a): held("w1_scale%d%d" % (b, a), [P, PASS], U8) for b in range(2) for a in range(2)}
         w4_codes = held("w4_codes", [P, PASSES, 2 * H], U8)
@@ -65,7 +68,6 @@ def tile_list_ad_bid_scores_kernel(
         bc_col = held("bc_col", [P, S2 // P], F32)
         v_codes = {}
         v2_codes = {}
-        v2_scale = {}
         w1_bf = {}
         a_bank = {}
         b_bank = {}
@@ -73,16 +75,20 @@ def tile_list_ad_bid_scores_kernel(
 
         def load_plane(plane, scales):
             for r in range(4):
-                nc.sync.dma_start(
+                nc.gpsimd.dma_start(
                     out=plane[r:P:32, :, :], in_=scales.bitcast(I32)[:, r:16:4, :].rearrange("a q n -> q a n")
                 )
 
         def load_tab2_plane():
-            for q in (0, 2, 1, 3):
-                nc.gpsimd.dma_start(
-                    out=tab2_plane[32 * q + 4 : 32 * q + 12, :],
-                    in_=tab2_scales.bitcast(I32)[:, 4 * q : 4 * q + 4, :],
-                )
+            nc.sync.dma_start(out=tab2_plane[0:P:4, :], in_=tab2_scales.bitcast(I32).rearrange("a s n -> (a s) n"))
+
+        def move_v2_scale():
+            for a in range(PASSES):
+                for r in range(4):
+                    nc.gpsimd.dma_start(
+                        out=v2_plane[4 * (a + 1) + r : P : 32, :],
+                        in_=v2_picked[64 * a + 4 * r : 64 * (a + 1) : 16, :].bitcast(I32),
+                    )
 
         def load_w1(b, a):
             rows = w1[a * PASS : (a + 1) * PASS, b * PASS : (b + 1) * PASS]
@@ -95,10 +101,14 @@ def tile_list_ad_bid_scores_kernel(
             nc.sync.dma_start(out=w4_raw[:], in_=w4_words.bitcast(I32).rearrange("a p n -> p a n"))
 
         def load_biases():
-            nc.gpsimd.dma_start(out=b1_col[:], in_=b1.rearrange("(b p t) -> p b t", b=PASSES, t=PACK))
-            nc.gpsimd.dma_start(out=bc_rows[0 : S2 // P, :], in_=bc.rearrange("(c p) -> c p", p=P))
+            nc.sync.dma_start(out=b1_rows[0:PASSES, :], in_=b1.rearrange("(b r) -> b r", b=PASSES))
+            nc.sync.dma_start(out=bc_rows[0 : S2 // P, :], in_=bc.rearrange("(c p) -> c p", p=P))
 
-        def turn_bc():
+        def turn_biases():
+            b1_bank = bank(6, [P, PACK, P])
+            for t in range(PACK):
+                nc.tensor.transpose(b1_bank[:, t, :], b1_rows[:, t:PASS:PACK], ident[:])
+            nc.scalar.copy(out=b1_col[:], in_=b1_bank[:, :, 0:PASSES])
             bc_bank = bank(7, [P, P])
             nc.tensor.transpose(bc_bank[:], bc_rows[:], ident[:])
             nc.scalar.copy(out=bc_col[:], in_=bc_bank[:, 0 : S2 // P])
@@ -130,11 +140,10 @@ def tile_list_ad_bid_scores_kernel(
             codes, at = v_codes[a, first // P]
             return codes[:, at : at + n].bitcast(FP8X4)
 
-        def gather_v2_scale(half, tag):
+        def gather_v2_scale(half):
             n = S2 // 2
-            v2_scale[half] = held("v2_scale%d" % half, [P, n], U8, tag)
             nc.vector.tensor_copy(
-                v2_scale[half][:],
+                v2_picked[:, half * n : (half + 1) * n],
                 tab2_plane[:].bitcast(U8).indirect(idx2[:, half * n // 16 : (half + 1) * n // 16]),
             )
 
@@ -184,7 +193,7 @@ def tile_list_ad_bid_scores_kernel(
                     out=a_sb[b, h][:, t, :],
                     in_=a_bank[b, h, t // 2][:, t % 2, :],
                     func=IDENTITY,
-                    bias=b1_col[:, b, t : t + 1],
+                    bias=b1_col[:, t, b : b + 1],
                 )
 
         def project_b(b, a, c):
@@ -229,7 +238,7 @@ def tile_list_ad_bid_scores_kernel(
                 nc.tensor.matmul_mx(
                     out=y_bank[c][:],
                     lhsT=v2_codes[b, half][:, cols].bitcast(FP8X4),
-                    lhsT_scale=v2_scale[half][4 * (b + 1) : P, cols],
+                    lhsT_scale=v2_plane[:].bitcast(U8)[4 * (b + 1) : P, c * P : (c + 1) * P],
                     rhs=h_codes[b][:].bitcast(FP8X4),
                     rhs_scale=h_scale[b][:],
                     start=(step == 0),
@@ -248,36 +257,41 @@ def tile_list_ad_bid_scores_kernel(
 
         on_scalar, on_vector = nc.scalar.copy, nc.vector.tensor_copy
 
-        nc.vector.memset(tab_planes[:], 0)
         nc.vector.memset(tab2_plane[:], 0)
-        nc.vector.memset(w4_plane[:], 0)
+        nc.vector.memset(b1_rows[:], 0.0)
         nc.vector.memset(bc_rows[:], 0.0)
+        nc.vector.memset(tab_planes[:], 0)
+        nc.vector.memset(w4_plane[:], 0)
+        nc.vector.memset(v2_plane[:], 0)
         make_identity(nc, ident[:])
-        load_tab2_plane()
-        load_biases()
-        load_w4()
-        nc.sync.dma_start(idx[:], offs)
-        nc.sync.dma_start(idx2[:], offs2)
         load_plane(tab_planes, tab_scales)
+        load_plane(w4_plane, w4_scales)
+        load_w4()
+        nc.sync.dma_start(idx2[:], offs2)
+        load_tab2_plane()
+        nc.sync.dma_start(idx[:], offs)
+        load_biases()
         load_w1(0, 0)
         load_words(tab_win[0], tab_words[0])
-        load_plane(w4_plane, w4_scales)
         load_w1(0, 1)
         load_words(tab_win[1], tab_words[1])
         load_w1(1, 0)
         load_w1(1, 1)
         load_words(tab2_win[0], tab2_words[0])
         load_words(tab2_win[1], tab2_words[1])
-
         permute_w4_codes()
+        gather_v2_scale(0)
+        gather_v2_scale(1)
+        move_v2_scale()
         gather_v_scale(0)
         gather_v_scale(1)
         round_w1(0, 0, 0, on_scalar)
         round_w1(0, 0, 1, on_scalar)
+        turn_biases()
         gather_v(0, 0, S)
-        permute_w4_scale()
         quantise_w1(0, 0, 0)
         quantise_w1(0, 0, 1)
+        permute_w4_scale()
         for h in range(2):
             project_a(0, 0, h)
         for c in range(4):
@@ -291,8 +305,6 @@ def tile_list_ad_bid_scores_kernel(
             project_a(0, 1, h)
             project_b(0, 1, 2 * h)
             project_b(0, 1, 2 * h + 1)
-        gather_v2_scale(0, "tab_win1")
-        gather_v2_scale(1, "tab_win0")
         add_b1(0, 0)
         round_w1(1, 0, 0, on_scalar)
         round_w1(1, 0, 1, on_scalar)
@@ -309,7 +321,6 @@ def tile_list_ad_bid_scores_kernel(
         interact(0, 2)
         interact(0, 3)
         quantise_h(0, 1)
-        turn_bc()
         for h in range(2):
             project_a(1, 0, h)
             project_a(1, 1, h)

@@ -43,7 +43,7 @@ def tile_list_ad_bid_scores_kernel(
         idx = lists.tile([P, S // 16], U16, name="idx")
         idx2 = lists.tile([P, S2 // 16], U16, name="idx2")
 
-        tab_planes = held("tab_planes", [P, PASSES, T // 4], I32)
+        tab_plane = held("tab_plane", [P, T // 4], I32)
         w4_plane = held("w4_plane", [P, PASSES, H // 4], I32)
         tab2_plane = held("tab2_plane", [P, T2 // 4], I32)
         bc_rows = held("bc_rows", [P, P], F32)
@@ -55,8 +55,9 @@ def tile_list_ad_bid_scores_kernel(
         w1_raw = {(b, a): held("w1_raw%d%d" % (b, a), [P, PACK, PASS], F32) for b in range(2) for a in range(2)}
         tab_win = [held("tab_win%d" % a, [P, T], I32) for a in range(2)]
         tab2_win = [held("tab2_win%d" % a, [P, T2], I32) for a in range(2)]
-        v_scale = [held("v_scale%d" % a, [P, S], U8) for a in range(2)]
-        w4_scale = held("w4_scale", [P, PASSES, H], U8, "tab_win0")
+        v_picked = held("v_picked", [P, S], U8)
+        v_plane = [held("v_plane%d" % a, [P, S // 4], I32) for a in range(PASSES)]
+        w4_scale = held("w4_scale", [P, PASSES, H], U8, "tab2_plane")
         w1_codes = {}
         w1_scale = {(b, a): held("w1_scale%d%d" % (b, a), [P, PASS], U8) for b in range(2) for a in range(2)}
         w4_codes = held("w4_codes", [P, PASSES, 2 * H], U8)
@@ -79,16 +80,15 @@ def tile_list_ad_bid_scores_kernel(
                     out=plane[r:P:32, :, :], in_=scales.bitcast(I32)[:, r:16:4, :].rearrange("a q n -> q a n")
                 )
 
-        def load_tab2_plane():
-            nc.sync.dma_start(out=tab2_plane[0:P:4, :], in_=tab2_scales.bitcast(I32).rearrange("a s n -> (a s) n"))
+        def load_spread(plane, scales):
+            nc.sync.dma_start(out=plane[0:P:4, :], in_=scales.bitcast(I32).rearrange("a s n -> (a s) n"))
 
-        def move_v2_scale():
-            for a in range(PASSES):
-                for r in range(4):
-                    nc.gpsimd.dma_start(
-                        out=v2_plane[4 * (a + 1) + r : P : 32, :],
-                        in_=v2_picked[64 * a + 4 * r : 64 * (a + 1) : 16, :].bitcast(I32),
-                    )
+        def move_scale(picked, a, plane, first):
+            for r in range(4):
+                nc.gpsimd.dma_start(
+                    out=plane[first + r : P : 32, :],
+                    in_=picked[64 * a + 4 * r : 64 * (a + 1) : 16, :].bitcast(I32),
+                )
 
         def load_w1(b, a):
             rows = w1[a * PASS : (a + 1) * PASS, b * PASS : (b + 1) * PASS]
@@ -125,8 +125,8 @@ def tile_list_ad_bid_scores_kernel(
                 in_=w4_plane[:].bitcast(U8).rearrange("p a (b m t) -> p (a b) t m", b=PASSES, t=PACK),
             )
 
-        def gather_v_scale(a):
-            nc.vector.tensor_copy(v_scale[a][:], tab_planes[:, a, :].bitcast(U8).indirect(idx[:]))
+        def gather_v_scale():
+            nc.vector.tensor_copy(v_picked[:], tab_plane[:].bitcast(U8).indirect(idx[:]))
 
         def gather_v(a, first, n):
             codes = held("v_codes%d_%d" % (a, first), [P, n], U32)
@@ -182,7 +182,7 @@ def tile_list_ad_bid_scores_kernel(
                         lhsT=w1_codes[b, a][:, cols].bitcast(FP8X4),
                         lhsT_scale=w1_scale[b, a][:, cols],
                         rhs=v_cols(a, h * HALF, HALF),
-                        rhs_scale=v_scale[a][:, js],
+                        rhs_scale=v_plane[a][:].bitcast(U8)[:, js],
                         start=(a == 0 and e == 0),
                         stop=(a == PASSES - 1 and e == 1),
                     )
@@ -207,7 +207,7 @@ def tile_list_ad_bid_scores_kernel(
                     lhsT=w4_codes[:, a, 2 * col : 2 * (col + P)].bitcast(FP4X4),
                     lhsT_scale=w4_scale[:, a, col : col + P],
                     rhs=v_cols(a, c * P, P),
-                    rhs_scale=v_scale[a][:, js],
+                    rhs_scale=v_plane[a][:].bitcast(U8)[:, js],
                     start=(a == 0 and t == 0),
                     stop=(a == PASSES - 1 and t == PACK - 1),
                 )
@@ -229,21 +229,19 @@ def tile_list_ad_bid_scores_kernel(
             js = slice(h * HALF, (h + 1) * HALF)
             nc.vector.quantize_mx(out=h_codes[b][:, js].bitcast(FP8X4), scales=h_scale[b][:, js], in_=h_bf[b, h][:])
 
-        def score(step, half):
-            b = step if half == 0 else 1 - step
-            for c in range(4 * half, 4 * half + 4):
-                if step == 0:
-                    y_bank[c] = bank(c, [P, S])
-                cols = slice((c % 4) * P, (c % 4 + 1) * P)
-                nc.tensor.matmul_mx(
-                    out=y_bank[c][:],
-                    lhsT=v2_codes[b, half][:, cols].bitcast(FP8X4),
-                    lhsT_scale=v2_plane[:].bitcast(U8)[4 * (b + 1) : P, c * P : (c + 1) * P],
-                    rhs=h_codes[b][:].bitcast(FP8X4),
-                    rhs_scale=h_scale[b][:],
-                    start=(step == 0),
-                    stop=(step == PASSES - 1),
-                )
+        def score(c, b, first):
+            if first:
+                y_bank[c] = bank(c, [P, S])
+            cols = slice((c % 4) * P, (c % 4 + 1) * P)
+            nc.tensor.matmul_mx(
+                out=y_bank[c][:],
+                lhsT=v2_codes[b, c // 4][:, cols].bitcast(FP8X4),
+                lhsT_scale=v2_plane[:].bitcast(U8)[4 * (b + 1) : P, c * P : (c + 1) * P],
+                rhs=h_codes[b][:].bitcast(FP8X4),
+                rhs_scale=h_scale[b][:],
+                start=first,
+                stop=not first,
+            )
 
         def store(c, on_vector):
             y_sb = held("y_sb%d" % c, [P, S], F32)
@@ -257,22 +255,24 @@ def tile_list_ad_bid_scores_kernel(
 
         on_scalar, on_vector = nc.scalar.copy, nc.vector.tensor_copy
 
+        nc.vector.memset(tab_plane[:], 0)
         nc.vector.memset(tab2_plane[:], 0)
-        nc.vector.memset(b1_rows[:], 0.0)
-        nc.vector.memset(bc_rows[:], 0.0)
-        nc.vector.memset(tab_planes[:], 0)
+        nc.gpsimd.memset(b1_rows[:], 0.0)
+        nc.gpsimd.memset(bc_rows[:], 0.0)
         nc.vector.memset(w4_plane[:], 0)
+        nc.vector.memset(v_plane[0][:], 0)
+        nc.vector.memset(v_plane[1][:], 0)
         nc.vector.memset(v2_plane[:], 0)
         make_identity(nc, ident[:])
-        load_plane(tab_planes, tab_scales)
         load_plane(w4_plane, w4_scales)
         load_w4()
-        nc.sync.dma_start(idx2[:], offs2)
-        load_tab2_plane()
         nc.sync.dma_start(idx[:], offs)
+        load_spread(tab_plane, tab_scales)
+        nc.sync.dma_start(idx2[:], offs2)
+        load_spread(tab2_plane, tab2_scales)
         load_biases()
-        load_w1(0, 0)
         load_words(tab_win[0], tab_words[0])
+        load_w1(0, 0)
         load_w1(0, 1)
         load_words(tab_win[1], tab_words[1])
         load_w1(1, 0)
@@ -280,11 +280,13 @@ def tile_list_ad_bid_scores_kernel(
         load_words(tab2_win[0], tab2_words[0])
         load_words(tab2_win[1], tab2_words[1])
         permute_w4_codes()
+        gather_v_scale()
+        for a in range(PASSES):
+            move_scale(v_picked, a, v_plane[a], 0)
         gather_v2_scale(0)
         gather_v2_scale(1)
-        move_v2_scale()
-        gather_v_scale(0)
-        gather_v_scale(1)
+        for a in range(PASSES):
+            move_scale(v2_picked, a, v2_plane, 4 * (a + 1))
         round_w1(0, 0, 0, on_scalar)
         round_w1(0, 0, 1, on_scalar)
         turn_biases()
@@ -292,10 +294,10 @@ def tile_list_ad_bid_scores_kernel(
         quantise_w1(0, 0, 0)
         quantise_w1(0, 0, 1)
         permute_w4_scale()
-        for h in range(2):
-            project_a(0, 0, h)
         for c in range(4):
             project_b(0, 0, c)
+        for h in range(2):
+            project_a(0, 0, h)
         round_w1(0, 1, 0, on_scalar)
         round_w1(0, 1, 1, on_vector)
         quantise_w1(0, 1, 1)
@@ -335,12 +337,18 @@ def tile_list_ad_bid_scores_kernel(
         interact(1, 3)
         gather_v2(0, 0)
         quantise_h(1, 1)
-        score(0, 0)
+        score(0, 0, True)
+        score(1, 0, True)
         gather_v2(1, 0)
-        score(1, 0)
+        score(0, 1, False)
+        score(1, 1, False)
+        for c in (2, 3):
+            score(c, 1, True)
+            score(c, 0, False)
         gather_v2(1, 1)
-        score(0, 1)
         gather_v2(0, 1)
-        score(1, 1)
+        for c in range(4, 8):
+            score(c, 1, True)
+            score(c, 0, False)
         for c in range(8):
             store(c, c in (5, 7))

@@ -80,12 +80,12 @@ def tile_list_ad_bid_scores_kernel(
                     out=plane[r:P:32, :, :], in_=scales.bitcast(I32)[:, r:16:4, :].rearrange("a q n -> q a n")
                 )
 
-        def load_spread(plane, scales):
-            nc.sync.dma_start(out=plane[0:P:4, :], in_=scales.bitcast(I32).rearrange("a s n -> (a s) n"))
+        def load_spread(queue, plane, scales):
+            queue.dma_start(out=plane[0:P:4, :], in_=scales.bitcast(I32).rearrange("a s n -> (a s) n"))
 
-        def move_scale(picked, a, plane, first):
+        def move_scale(queue, picked, a, plane, first):
             for r in range(4):
-                nc.gpsimd.dma_start(
+                queue.dma_start(
                     out=plane[first + r : P : 32, :],
                     in_=picked[64 * a + 4 * r : 64 * (a + 1) : 16, :].bitcast(I32),
                 )
@@ -100,9 +100,9 @@ def tile_list_ad_bid_scores_kernel(
         def load_w4():
             nc.sync.dma_start(out=w4_raw[:], in_=w4_words.bitcast(I32).rearrange("a p n -> p a n"))
 
-        def load_biases():
-            nc.sync.dma_start(out=b1_rows[0:PASSES, :], in_=b1.rearrange("(b r) -> b r", b=PASSES))
-            nc.sync.dma_start(out=bc_rows[0 : S2 // P, :], in_=bc.rearrange("(c p) -> c p", p=P))
+        def load_biases(queue):
+            queue.dma_start(out=b1_rows[0:PASSES, :], in_=b1.rearrange("(b r) -> b r", b=PASSES))
+            queue.dma_start(out=bc_rows[0 : S2 // P, :], in_=bc.rearrange("(c p) -> c p", p=P))
 
         def turn_biases():
             b1_bank = bank(6, [P, PACK, P])
@@ -258,7 +258,6 @@ def tile_list_ad_bid_scores_kernel(
         nc.vector.memset(tab_plane[:], 0)
         nc.vector.memset(tab2_plane[:], 0)
         nc.gpsimd.memset(b1_rows[:], 0.0)
-        nc.gpsimd.memset(bc_rows[:], 0.0)
         nc.vector.memset(w4_plane[:], 0)
         nc.vector.memset(v_plane[0][:], 0)
         nc.vector.memset(v_plane[1][:], 0)
@@ -267,11 +266,12 @@ def tile_list_ad_bid_scores_kernel(
         load_plane(w4_plane, w4_scales)
         load_w4()
         nc.sync.dma_start(idx[:], offs)
-        load_spread(tab_plane, tab_scales)
-        nc.sync.dma_start(idx2[:], offs2)
-        load_spread(tab2_plane, tab2_scales)
-        load_biases()
+        load_spread(nc.scalar, tab_plane, tab_scales)
+        load_spread(nc.scalar, tab2_plane, tab2_scales)
+        nc.scalar.copy(out=bc_rows[:], in_=b1_rows[:, 0:P])
         load_words(tab_win[0], tab_words[0])
+        nc.sync.dma_start(idx2[:], offs2)
+        load_biases(nc.scalar)
         load_w1(0, 0)
         load_w1(0, 1)
         load_words(tab_win[1], tab_words[1])
@@ -282,11 +282,11 @@ def tile_list_ad_bid_scores_kernel(
         permute_w4_codes()
         gather_v_scale()
         for a in range(PASSES):
-            move_scale(v_picked, a, v_plane[a], 0)
+            move_scale(nc.scalar, v_picked, a, v_plane[a], 0)
         gather_v2_scale(0)
         gather_v2_scale(1)
         for a in range(PASSES):
-            move_scale(v2_picked, a, v2_plane, 4 * (a + 1))
+            move_scale(nc.gpsimd, v2_picked, a, v2_plane, 4 * (a + 1))
         round_w1(0, 0, 0, on_scalar)
         round_w1(0, 0, 1, on_scalar)
         turn_biases()

@@ -100,9 +100,11 @@ def tile_list_ad_bid_scores_kernel(
         def load_w4():
             nc.sync.dma_start(out=w4_raw[:], in_=w4_words.bitcast(I32).rearrange("a p n -> p a n"))
 
-        def load_biases(queue):
-            queue.dma_start(out=b1_rows[0:PASSES, :], in_=b1.rearrange("(b r) -> b r", b=PASSES))
-            queue.dma_start(out=bc_rows[0 : S2 // P, :], in_=bc.rearrange("(c p) -> c p", p=P))
+        def load_b1():
+            nc.scalar.dma_start(out=b1_rows[0:PASSES, :], in_=b1.rearrange("(b r) -> b r", b=PASSES))
+
+        def load_bc():
+            nc.scalar.dma_start(out=bc_rows[0 : S2 // P, :], in_=bc.rearrange("(c p) -> c p", p=P))
 
         def turn_biases():
             b1_bank = bank(6, [P, PACK, P])
@@ -187,14 +189,15 @@ def tile_list_ad_bid_scores_kernel(
                         stop=(a == PASSES - 1 and e == 1),
                     )
 
-        def add_b1(b, h):
-            for t in range(PACK):
-                nc.scalar.activation(
-                    out=a_sb[b, h][:, t, :],
-                    in_=a_bank[b, h, t // 2][:, t % 2, :],
-                    func=IDENTITY,
-                    bias=b1_col[:, t, b : b + 1],
-                )
+        def add_b1(b, h, width):
+            for j in range(0, HALF, width):
+                for t in range(PACK):
+                    nc.scalar.activation(
+                        out=a_sb[b, h][:, t, j : j + width],
+                        in_=a_bank[b, h, t // 2][:, t % 2, j : j + width],
+                        func=IDENTITY,
+                        bias=b1_col[:, t, b : b + 1],
+                    )
 
         def project_b(b, a, c):
             if a == 0:
@@ -268,10 +271,11 @@ def tile_list_ad_bid_scores_kernel(
         nc.sync.dma_start(idx[:], offs)
         load_spread(nc.scalar, tab_plane, tab_scales)
         load_spread(nc.scalar, tab2_plane, tab2_scales)
-        nc.scalar.copy(out=bc_rows[:], in_=b1_rows[:, 0:P])
+        load_b1()
+        nc.scalar.copy(out=bc_rows[:], in_=ident[:])
+        load_bc()
         load_words(tab_win[0], tab_words[0])
         nc.sync.dma_start(idx2[:], offs2)
-        load_biases(nc.scalar)
         load_w1(0, 0)
         load_w1(0, 1)
         load_words(tab_win[1], tab_words[1])
@@ -281,8 +285,8 @@ def tile_list_ad_bid_scores_kernel(
         load_words(tab2_win[1], tab2_words[1])
         permute_w4_codes()
         gather_v_scale()
-        for a in range(PASSES):
-            move_scale(nc.scalar, v_picked, a, v_plane[a], 0)
+        move_scale(nc.scalar, v_picked, 0, v_plane[0], 0)
+        move_scale(nc.gpsimd, v_picked, 1, v_plane[1], 0)
         gather_v2_scale(0)
         gather_v2_scale(1)
         for a in range(PASSES):
@@ -307,26 +311,26 @@ def tile_list_ad_bid_scores_kernel(
             project_a(0, 1, h)
             project_b(0, 1, 2 * h)
             project_b(0, 1, 2 * h + 1)
-        add_b1(0, 0)
+        add_b1(0, 0, P)
         round_w1(1, 0, 0, on_scalar)
-        round_w1(1, 0, 1, on_scalar)
-        add_b1(0, 1)
+        round_w1(1, 1, 0, on_scalar)
+        add_b1(0, 1, HALF)
         interact(0, 0)
         interact(0, 1)
         quantise_h(0, 0)
-        round_w1(1, 1, 0, on_vector)
+        round_w1(1, 0, 1, on_vector)
         round_w1(1, 1, 1, on_vector)
         quantise_w1(1, 0, 0)
-        quantise_w1(1, 1, 0)
         quantise_w1(1, 0, 1)
         quantise_w1(1, 1, 1)
+        quantise_w1(1, 1, 0)
         interact(0, 2)
         interact(0, 3)
         quantise_h(0, 1)
         for h in range(2):
             project_a(1, 0, h)
             project_a(1, 1, h)
-            add_b1(1, h)
+            add_b1(1, h, HALF)
         for c in range(4):
             project_b(1, 0, c)
             project_b(1, 1, c)

@@ -246,6 +246,19 @@ def tile_list_ad_bid_scores_kernel(
                 stop=not first,
             )
 
+        def warm_up(passes):
+            spare = bank(7, [P, S])
+            for n in range(passes):
+                nc.tensor.matmul_mx(
+                    out=spare[:],
+                    lhsT=w1_codes[1, 1][:, 0:P].bitcast(FP8X4),
+                    lhsT_scale=w1_scale[1, 1][:, 0:P],
+                    rhs=v_cols(0, 0, S),
+                    rhs_scale=v_plane[0][:].bitcast(U8),
+                    start=True,
+                    stop=True,
+                )
+
         def store(c, on_vector):
             y_sb = held("y_sb%d" % c, [P, S], F32)
             if on_vector:
@@ -339,6 +352,7 @@ def tile_list_ad_bid_scores_kernel(
         interact(1, 2)
         quantise_h(1, 0)
         interact(1, 3)
+        warm_up(3)
         gather_v2(0, 0)
         quantise_h(1, 1)
         score(0, 0, True)

@@ -23,6 +23,7 @@ PACK = 4
 PASS = P * PACK
 PASSES = 2
 HALF = S // 2
+ROW = S + H + S2
 
 
 def tile_list_ad_bid_scores_kernel(
@@ -44,26 +45,25 @@ def tile_list_ad_bid_scores_kernel(
         idx2 = lists.tile([P, S2 // 16], U16, name="idx2")
 
         tab_plane = held("tab_plane", [P, T // 4], I32)
-        w4_plane = held("w4_plane", [P, PASSES, H // 4], I32)
+        w4_plane = held("w4_plane", [P, H // 4], I32)
         tab2_plane = held("tab2_plane", [P, T2 // 4], I32)
         bc_rows = held("bc_rows", [P, P], F32)
         b1_rows = held("b1_rows", [P, PASS], F32)
-        v2_plane = held("v2_plane", [P, S2 // 4], I32)
         v2_picked = held("v2_picked", [P, S2], U8)
         w4_raw = held("w4_raw", [P, PASSES, H // 2], I32)
         b1_col = held("b1_col", [P, PACK, PASSES], F32)
-        w1_raw = {(b, a): held("w1_raw%d%d" % (b, a), [P, PACK, PASS], F32) for b in range(2) for a in range(2)}
+        w1_raw = {}
         tab_win = [held("tab_win%d" % a, [P, T], I32) for a in range(2)]
         tab2_win = [held("tab2_win%d" % a, [P, T2], I32) for a in range(2)]
         v_picked = held("v_picked", [P, S], U8)
-        v_plane = [held("v_plane%d" % a, [P, S // 4], I32) for a in range(PASSES)]
-        w4_scale = held("w4_scale", [P, PASSES, H], U8, "tab2_plane")
+        staged = held("staged", [P, ROW], U8)
+        planes = [held("planes%d" % a, [P, ROW // 4], I32) for a in range(PASSES)]
         w1_codes = {}
         w1_scale = {(b, a): held("w1_scale%d%d" % (b, a), [P, PASS], U8) for b in range(2) for a in range(2)}
         w4_codes = held("w4_codes", [P, PASSES, 2 * H], U8)
         h_codes = {}
         h_scale = [held("h_scale%d" % b, [P, S], U8) for b in range(2)]
-        a_sb = {(b, h): held("a_sb%d%d" % (b, h), [P, PACK, HALF], F32) for b in range(2) for h in range(2)}
+        a_sb = {}
         h_bf = {}
         ident = held("ident", [P, P], F32)
         bc_col = held("bc_col", [P, S2 // P], F32)
@@ -74,25 +74,24 @@ def tile_list_ad_bid_scores_kernel(
         b_bank = {}
         y_bank = {}
 
-        def load_plane(plane, scales):
-            for r in range(4):
-                nc.gpsimd.dma_start(
-                    out=plane[r:P:32, :, :], in_=scales.bitcast(I32)[:, r:16:4, :].rearrange("a q n -> q a n")
-                )
-
         def load_spread(queue, plane, scales):
             queue.dma_start(out=plane[0:P:4, :], in_=scales.bitcast(I32).rearrange("a s n -> (a s) n"))
 
-        def move_scale(queue, picked, a, plane, first):
+        def move_scale(queue, a):
             for r in range(4):
                 queue.dma_start(
-                    out=plane[first + r : P : 32, :],
-                    in_=picked[64 * a + 4 * r : 64 * (a + 1) : 16, :].bitcast(I32),
+                    out=planes[a][r:P:32, :], in_=staged[64 * a + 4 * r : 64 * (a + 1) : 16, :].bitcast(I32)
                 )
 
-        def load_w1(b, a):
-            rows = w1[a * PASS : (a + 1) * PASS, b * PASS : (b + 1) * PASS]
-            nc.sync.dma_start(out=w1_raw[b, a][:], in_=rows.rearrange("(p j) c -> p j c", j=PACK))
+        def stage(picked, at, n):
+            nc.vector.tensor_copy(out=staged[:, at : at + n].bitcast(I32), in_=picked[:].bitcast(I32))
+
+        def load_w1(a, first, n):
+            raw = held("w1_raw%d%d" % (a, first), [P, PACK, n * PASS], F32)
+            rows = w1[a * PASS : (a + 1) * PASS, first * PASS : (first + n) * PASS]
+            nc.sync.dma_start(out=raw[:], in_=rows.rearrange("(p j) c -> p j c", j=PACK))
+            for b in range(first, first + n):
+                w1_raw[b, a] = raw[:, :, (b - first) * PASS : (b - first + 1) * PASS]
 
         def load_words(win, words):
             nc.sync.dma_start(out=win[:], in_=words.rearrange("p t i -> p (t i)").bitcast(I32))
@@ -123,8 +122,8 @@ def tile_list_ad_bid_scores_kernel(
 
         def permute_w4_scale():
             nc.vector.tensor_copy(
-                out=w4_scale[:].rearrange("p a (b t m) -> p (a b) t m", b=PASSES, t=PACK),
-                in_=w4_plane[:].bitcast(U8).rearrange("p a (b m t) -> p (a b) t m", b=PASSES, t=PACK),
+                out=staged[:, S : S + H].rearrange("p (b t m) -> p b t m", b=PASSES, t=PACK),
+                in_=w4_plane[:].bitcast(U8).rearrange("p (b m t) -> p b t m", b=PASSES, t=PACK),
             )
 
         def gather_v_scale():
@@ -161,7 +160,7 @@ def tile_list_ad_bid_scores_kernel(
             w1_bf[b, a, u] = held("w1_bf%d%d%d" % (b, a, u), [P, PASS * 2], BF16)
             copy(
                 out=w1_bf[b, a, u][:].rearrange("p (t m j) -> p m j t", t=2, j=PACK),
-                in_=w1_raw[b, a][:].rearrange("p j (m t) -> p m j t", t=PACK)[:, :, :, 2 * u : 2 * u + 2],
+                in_=w1_raw[b, a].rearrange("p j (m t) -> p m j t", t=PACK)[:, :, :, 2 * u : 2 * u + 2],
             )
 
         def quantise_w1(b, a, u):
@@ -184,12 +183,13 @@ def tile_list_ad_bid_scores_kernel(
                         lhsT=w1_codes[b, a][:, cols].bitcast(FP8X4),
                         lhsT_scale=w1_scale[b, a][:, cols],
                         rhs=v_cols(a, h * HALF, HALF),
-                        rhs_scale=v_plane[a][:].bitcast(U8)[:, js],
+                        rhs_scale=planes[a][:].bitcast(U8)[:, js],
                         start=(a == 0 and e == 0),
                         stop=(a == PASSES - 1 and e == 1),
                     )
 
-        def add_b1(b, h, width):
+        def add_b1(b, h, width, tag=None):
+            a_sb[b, h] = held("a_sb%d%d" % (b, h), [P, PACK, HALF], F32, tag)
             for j in range(0, HALF, width):
                 for t in range(PACK):
                     nc.scalar.activation(
@@ -208,9 +208,9 @@ def tile_list_ad_bid_scores_kernel(
                 nc.tensor.matmul_mx(
                     out=b_bank[b, c][:, t, :],
                     lhsT=w4_codes[:, a, 2 * col : 2 * (col + P)].bitcast(FP4X4),
-                    lhsT_scale=w4_scale[:, a, col : col + P],
+                    lhsT_scale=planes[a][:].bitcast(U8)[:, S + col : S + col + P],
                     rhs=v_cols(a, c * P, P),
-                    rhs_scale=v_plane[a][:].bitcast(U8)[:, js],
+                    rhs_scale=planes[a][:].bitcast(U8)[:, js],
                     start=(a == 0 and t == 0),
                     stop=(a == PASSES - 1 and t == PACK - 1),
                 )
@@ -218,7 +218,7 @@ def tile_list_ad_bid_scores_kernel(
         def interact(b, c):
             h, at = c // 2, (c % 2) * P
             if at == 0:
-                h_bf[b, h] = held("h_bf%d%d" % (b, h), [P, HALF * PACK], BF16, "w1_bf111" if (b, h) == (0, 1) else None)
+                h_bf[b, h] = held("h_bf%d%d" % (b, h), [P, HALF * PACK], BF16)
             nc.vector.tensor_tensor(
                 out=h_bf[b, h][:, at * PACK : (at + P) * PACK].rearrange("p (g i t) -> p g t i", i=4, t=PACK),
                 in0=b_bank[b, c][:].rearrange("p t (g i) -> p g t i", i=4),
@@ -239,7 +239,7 @@ def tile_list_ad_bid_scores_kernel(
             nc.tensor.matmul_mx(
                 out=y_bank[c][:],
                 lhsT=v2_codes[b, c // 4][:, cols].bitcast(FP8X4),
-                lhsT_scale=v2_plane[:].bitcast(U8)[4 * (b + 1) : P, c * P : (c + 1) * P],
+                lhsT_scale=planes[b][:].bitcast(U8)[:, S + H + c * P : S + H + (c + 1) * P],
                 rhs=h_codes[b][:].bitcast(FP8X4),
                 rhs_scale=h_scale[b][:],
                 start=first,
@@ -254,7 +254,7 @@ def tile_list_ad_bid_scores_kernel(
                     lhsT=w1_codes[1, 1][:, 0:P].bitcast(FP8X4),
                     lhsT_scale=w1_scale[1, 1][:, 0:P],
                     rhs=v_cols(0, 0, S),
-                    rhs_scale=v_plane[0][:].bitcast(U8),
+                    rhs_scale=planes[0][:].bitcast(U8)[:, 0:S],
                     start=True,
                     stop=True,
                 )
@@ -273,52 +273,51 @@ def tile_list_ad_bid_scores_kernel(
 
         nc.vector.memset(tab_plane[:], 0)
         nc.vector.memset(tab2_plane[:], 0)
-        nc.gpsimd.memset(b1_rows[:], 0.0)
         nc.vector.memset(w4_plane[:], 0)
-        nc.vector.memset(v_plane[0][:], 0)
-        nc.vector.memset(v_plane[1][:], 0)
-        nc.vector.memset(v2_plane[:], 0)
+        nc.vector.memset(planes[0][:], 0)
+        nc.vector.memset(planes[1][:], 0)
+        nc.vector.memset(b1_rows[:], 0.0)
         make_identity(nc, ident[:])
-        load_plane(w4_plane, w4_scales)
-        load_w4()
         nc.sync.dma_start(idx[:], offs)
+        nc.sync.dma_start(idx2[:], offs2)
         load_spread(nc.scalar, tab_plane, tab_scales)
         load_spread(nc.scalar, tab2_plane, tab2_scales)
-        load_b1()
+        load_spread(nc.scalar, w4_plane, w4_scales)
         nc.scalar.copy(out=bc_rows[:], in_=ident[:])
-        load_bc()
+        load_w1(0, 0, 1)
         load_words(tab_win[0], tab_words[0])
-        nc.sync.dma_start(idx2[:], offs2)
-        load_w1(0, 0)
-        load_w1(0, 1)
+        load_w4()
+        load_w1(1, 0, 1)
         load_words(tab_win[1], tab_words[1])
-        load_w1(1, 0)
-        load_w1(1, 1)
+        load_w1(0, 1, 1)
+        load_w1(1, 1, 1)
         load_words(tab2_win[0], tab2_words[0])
         load_words(tab2_win[1], tab2_words[1])
-        permute_w4_codes()
         gather_v_scale()
-        move_scale(nc.scalar, v_picked, 0, v_plane[0], 0)
-        move_scale(nc.gpsimd, v_picked, 1, v_plane[1], 0)
         gather_v2_scale(0)
+        stage(v_picked, 0, S)
         gather_v2_scale(1)
-        for a in range(PASSES):
-            move_scale(nc.gpsimd, v2_picked, a, v2_plane, 4 * (a + 1))
+        permute_w4_scale()
+        stage(v2_picked, S + H, S2)
+        load_b1()
+        load_bc()
+        move_scale(nc.scalar, 0)
         round_w1(0, 0, 0, on_scalar)
         round_w1(0, 0, 1, on_scalar)
+        move_scale(nc.gpsimd, 1)
         turn_biases()
         gather_v(0, 0, S)
         quantise_w1(0, 0, 0)
         quantise_w1(0, 0, 1)
-        permute_w4_scale()
-        for c in range(4):
-            project_b(0, 0, c)
-        for h in range(2):
-            project_a(0, 0, h)
+        permute_w4_codes()
         round_w1(0, 1, 0, on_scalar)
         round_w1(0, 1, 1, on_vector)
         quantise_w1(0, 1, 1)
         quantise_w1(0, 1, 0)
+        for h in range(2):
+            project_a(0, 0, h)
+        for c in range(4):
+            project_b(0, 0, c)
         for h in range(2):
             gather_v(1, h * HALF, HALF)
             project_a(0, 1, h)
@@ -327,42 +326,39 @@ def tile_list_ad_bid_scores_kernel(
         add_b1(0, 0, P)
         round_w1(1, 0, 0, on_scalar)
         round_w1(1, 1, 0, on_scalar)
-        add_b1(0, 1, HALF)
+        round_w1(1, 0, 1, on_vector)
+        round_w1(1, 1, 1, on_vector)
+        add_b1(0, 1, HALF, "w1_raw11")
+        quantise_w1(1, 0, 1)
+        quantise_w1(1, 0, 0)
+        quantise_w1(1, 1, 1)
+        quantise_w1(1, 1, 0)
         interact(0, 0)
         interact(0, 1)
         quantise_h(0, 0)
-        round_w1(1, 0, 1, on_vector)
-        round_w1(1, 1, 1, on_vector)
-        quantise_w1(1, 0, 0)
-        quantise_w1(1, 0, 1)
-        quantise_w1(1, 1, 1)
-        quantise_w1(1, 1, 0)
         interact(0, 2)
         interact(0, 3)
         quantise_h(0, 1)
         for h in range(2):
             project_a(1, 0, h)
             project_a(1, 1, h)
-            add_b1(1, h, HALF)
-        for c in range(4):
-            project_b(1, 0, c)
-            project_b(1, 1, c)
+            add_b1(1, h, P if h == 0 else HALF)
+            for c in (2 * h, 2 * h + 1):
+                project_b(1, 0, c)
+                project_b(1, 1, c)
+        gather_v2(0, 0)
         interact(1, 0)
         interact(1, 1)
         interact(1, 2)
         quantise_h(1, 0)
         interact(1, 3)
-        warm_up(3)
-        gather_v2(0, 0)
         quantise_h(1, 1)
-        score(0, 0, True)
-        score(1, 0, True)
+        for c in range(4):
+            score(c, 0, True)
+        warm_up(2)
         gather_v2(1, 0)
-        score(0, 1, False)
-        score(1, 1, False)
-        for c in (2, 3):
-            score(c, 1, True)
-            score(c, 0, False)
+        for c in range(4):
+            score(c, 1, False)
         gather_v2(1, 1)
         gather_v2(0, 1)
         for c in range(4, 8):

@@ -23,7 +23,7 @@ PACK = 4
 PASS = P * PACK
 PASSES = 2
 HALF = S // 2
-ROW = S + H + S2
+ROW = S + H
 
 
 def tile_list_ad_bid_scores_kernel(
@@ -51,13 +51,13 @@ def tile_list_ad_bid_scores_kernel(
         b1_rows = held("b1_rows", [P, PASS], F32)
         v2_picked = held("v2_picked", [P, S2], U8)
         w4_raw = held("w4_raw", [P, PASSES, H // 2], I32)
-        b1_col = held("b1_col", [P, PACK, PASSES], F32)
         w1_raw = {}
         tab_win = [held("tab_win%d" % a, [P, T], I32) for a in range(2)]
         tab2_win = [held("tab2_win%d" % a, [P, T2], I32) for a in range(2)]
         v_picked = held("v_picked", [P, S], U8)
         staged = held("staged", [P, ROW], U8)
-        planes = [held("planes%d" % a, [P, ROW // 4], I32) for a in range(PASSES)]
+        v2_plane = held("v2_plane", [P, PASSES, S2 // 4], I32)
+        planes = held("planes", [P, PASSES, ROW // 4], I32)
         w1_codes = {}
         w1_scale = {(b, a): held("w1_scale%d%d" % (b, a), [P, PASS], U8) for b in range(2) for a in range(2)}
         w4_codes = held("w4_codes", [P, PASSES, 2 * H], U8)
@@ -66,7 +66,6 @@ def tile_list_ad_bid_scores_kernel(
         a_sb = {}
         h_bf = {}
         ident = held("ident", [P, P], F32)
-        bc_col = held("bc_col", [P, S2 // P], F32)
         v_codes = {}
         v2_codes = {}
         w1_bf = {}
@@ -75,12 +74,13 @@ def tile_list_ad_bid_scores_kernel(
         y_bank = {}
 
         def load_spread(queue, plane, scales):
-            queue.dma_start(out=plane[0:P:4, :], in_=scales.bitcast(I32).rearrange("a s n -> (a s) n"))
+            queue.dma_start(out=plane[0:P:4, :], in_=scales.bitcast(I32).rearrange("a s n -> s a n"))
 
-        def move_scale(queue, a):
-            for r in range(4):
+        def move_scale(queue, plane, first, rows):
+            for q in range(4):
                 queue.dma_start(
-                    out=planes[a][r:P:32, :], in_=staged[64 * a + 4 * r : 64 * (a + 1) : 16, :].bitcast(I32)
+                    out=plane[32 * q + first : 32 * q + first + 4, :, :],
+                    in_=rows[32 * q : 32 * (q + 1) : 4, :].bitcast(I32),
                 )
 
         def stage(picked, at, n):
@@ -100,19 +100,21 @@ def tile_list_ad_bid_scores_kernel(
             nc.sync.dma_start(out=w4_raw[:], in_=w4_words.bitcast(I32).rearrange("a p n -> p a n"))
 
         def load_b1():
-            nc.scalar.dma_start(out=b1_rows[0:PASSES, :], in_=b1.rearrange("(b r) -> b r", b=PASSES))
+            nc.sync.dma_start(out=b1_rows[0:PASSES, :], in_=b1.rearrange("(b r) -> b r", b=PASSES))
 
         def load_bc():
-            nc.scalar.dma_start(out=bc_rows[0 : S2 // P, :], in_=bc.rearrange("(c p) -> c p", p=P))
+            nc.sync.dma_start(out=bc_rows[0 : S2 // P, :], in_=bc.rearrange("(c p) -> c p", p=P))
 
-        def turn_biases():
+        def turn_biases(tag):
+            both = held("bias_cols", [P, 2, PACK * PASSES], F32, tag)
             b1_bank = bank(6, [P, PACK, P])
             for t in range(PACK):
                 nc.tensor.transpose(b1_bank[:, t, :], b1_rows[:, t:PASS:PACK], ident[:])
-            nc.scalar.copy(out=b1_col[:], in_=b1_bank[:, :, 0:PASSES])
+            nc.scalar.copy(out=both[:, 0, :].rearrange("p (t b) -> p t b", b=PASSES), in_=b1_bank[:, :, 0:PASSES])
             bc_bank = bank(7, [P, P])
             nc.tensor.transpose(bc_bank[:], bc_rows[:], ident[:])
-            nc.scalar.copy(out=bc_col[:], in_=bc_bank[:, 0 : S2 // P])
+            nc.scalar.copy(out=both[:, 1, :], in_=bc_bank[:, 0 : S2 // P])
+            return both
 
         def permute_w4_codes():
             nc.vector.tensor_copy(
@@ -183,21 +185,23 @@ def tile_list_ad_bid_scores_kernel(
                         lhsT=w1_codes[b, a][:, cols].bitcast(FP8X4),
                         lhsT_scale=w1_scale[b, a][:, cols],
                         rhs=v_cols(a, h * HALF, HALF),
-                        rhs_scale=planes[a][:].bitcast(U8)[:, js],
+                        rhs_scale=planes[:].bitcast(U8)[:, a, js],
                         start=(a == 0 and e == 0),
                         stop=(a == PASSES - 1 and e == 1),
                     )
 
-        def add_b1(b, h, width, tag=None):
-            a_sb[b, h] = held("a_sb%d%d" % (b, h), [P, PACK, HALF], F32, tag)
-            for j in range(0, HALF, width):
-                for t in range(PACK):
-                    nc.scalar.activation(
-                        out=a_sb[b, h][:, t, j : j + width],
-                        in_=a_bank[b, h, t // 2][:, t % 2, j : j + width],
-                        func=IDENTITY,
-                        bias=b1_col[:, t, b : b + 1],
-                    )
+        def add_b1(b, c, n, tag=None):
+            sums = held("a_sb%d%d" % (b, c), [P, PACK, n * P], F32, tag)
+            at = (c % 2) * P
+            for t in range(PACK):
+                nc.scalar.activation(
+                    out=sums[:, t, :],
+                    in_=a_bank[b, c // 2, t // 2][:, t % 2, at : at + n * P],
+                    func=IDENTITY,
+                    bias=bias_cols[:, 0, PASSES * t + b : PASSES * t + b + 1],
+                )
+            for e in range(n):
+                a_sb[b, c + e] = sums[:, :, e * P : (e + 1) * P]
 
         def project_b(b, a, c):
             if a == 0:
@@ -208,9 +212,9 @@ def tile_list_ad_bid_scores_kernel(
                 nc.tensor.matmul_mx(
                     out=b_bank[b, c][:, t, :],
                     lhsT=w4_codes[:, a, 2 * col : 2 * (col + P)].bitcast(FP4X4),
-                    lhsT_scale=planes[a][:].bitcast(U8)[:, S + col : S + col + P],
+                    lhsT_scale=planes[:].bitcast(U8)[:, a, S + col : S + col + P],
                     rhs=v_cols(a, c * P, P),
-                    rhs_scale=planes[a][:].bitcast(U8)[:, js],
+                    rhs_scale=planes[:].bitcast(U8)[:, a, js],
                     start=(a == 0 and t == 0),
                     stop=(a == PASSES - 1 and t == PACK - 1),
                 )
@@ -222,7 +226,7 @@ def tile_list_ad_bid_scores_kernel(
             nc.vector.tensor_tensor(
                 out=h_bf[b, h][:, at * PACK : (at + P) * PACK].rearrange("p (g i t) -> p g t i", i=4, t=PACK),
                 in0=b_bank[b, c][:].rearrange("p t (g i) -> p g t i", i=4),
-                in1=a_sb[b, h][:, :, at : at + P].rearrange("p t (g i) -> p g t i", i=4),
+                in1=a_sb[b, c].rearrange("p t (g i) -> p g t i", i=4),
                 op=MULT,
             )
 
@@ -239,7 +243,7 @@ def tile_list_ad_bid_scores_kernel(
             nc.tensor.matmul_mx(
                 out=y_bank[c][:],
                 lhsT=v2_codes[b, c // 4][:, cols].bitcast(FP8X4),
-                lhsT_scale=planes[b][:].bitcast(U8)[:, S + H + c * P : S + H + (c + 1) * P],
+                lhsT_scale=v2_plane[:].bitcast(U8)[4:P, b, c * P : (c + 1) * P],
                 rhs=h_codes[b][:].bitcast(FP8X4),
                 rhs_scale=h_scale[b][:],
                 start=first,
@@ -254,7 +258,7 @@ def tile_list_ad_bid_scores_kernel(
                     lhsT=w1_codes[1, 1][:, 0:P].bitcast(FP8X4),
                     lhsT_scale=w1_scale[1, 1][:, 0:P],
                     rhs=v_cols(0, 0, S),
-                    rhs_scale=planes[0][:].bitcast(U8)[:, 0:S],
+                    rhs_scale=planes[:].bitcast(U8)[:, 0, 0:S],
                     start=True,
                     stop=True,
                 )
@@ -263,53 +267,52 @@ def tile_list_ad_bid_scores_kernel(
             y_sb = held("y_sb%d" % c, [P, S], F32)
             if on_vector:
                 nc.vector.tensor_scalar(
-                    out=y_sb[:], in0=y_bank[c][:], scalar1=bc_col[:, c : c + 1], scalar2=None, op0=ADD
+                    out=y_sb[:], in0=y_bank[c][:], scalar1=bias_cols[:, 1, c : c + 1], scalar2=None, op0=ADD
                 )
             else:
-                nc.scalar.activation(out=y_sb[:], in_=y_bank[c][:], func=IDENTITY, bias=bc_col[:, c : c + 1])
+                nc.scalar.activation(out=y_sb[:], in_=y_bank[c][:], func=IDENTITY, bias=bias_cols[:, 1, c : c + 1])
             nc.sync.dma_start(out=out[c * P : (c + 1) * P, :], in_=y_sb[:])
 
         on_scalar, on_vector = nc.scalar.copy, nc.vector.tensor_copy
 
         nc.vector.memset(tab_plane[:], 0)
-        nc.vector.memset(tab2_plane[:], 0)
         nc.vector.memset(w4_plane[:], 0)
-        nc.vector.memset(planes[0][:], 0)
-        nc.vector.memset(planes[1][:], 0)
+        nc.vector.memset(tab2_plane[:], 0)
+        nc.vector.memset(planes[:], 0)
+        nc.vector.memset(v2_plane[:], 0)
         nc.vector.memset(b1_rows[:], 0.0)
         make_identity(nc, ident[:])
+        load_w4()
         nc.sync.dma_start(idx[:], offs)
-        nc.sync.dma_start(idx2[:], offs2)
-        load_spread(nc.scalar, tab_plane, tab_scales)
-        load_spread(nc.scalar, tab2_plane, tab2_scales)
-        load_spread(nc.scalar, w4_plane, w4_scales)
+        load_spread(nc.sync, tab_plane, tab_scales)
+        load_spread(nc.sync, w4_plane, w4_scales)
         nc.scalar.copy(out=bc_rows[:], in_=ident[:])
         load_w1(0, 0, 1)
+        nc.sync.dma_start(idx2[:], offs2)
+        load_spread(nc.sync, tab2_plane, tab2_scales)
         load_words(tab_win[0], tab_words[0])
-        load_w4()
+        load_b1()
+        load_bc()
         load_w1(1, 0, 1)
+        permute_w4_codes()
+        gather_v_scale()
+        permute_w4_scale()
+        stage(v_picked, 0, S)
+        move_scale(nc.sync, planes, 0, staged)
         load_words(tab_win[1], tab_words[1])
         load_w1(0, 1, 1)
         load_w1(1, 1, 1)
         load_words(tab2_win[0], tab2_words[0])
         load_words(tab2_win[1], tab2_words[1])
-        gather_v_scale()
         gather_v2_scale(0)
-        stage(v_picked, 0, S)
         gather_v2_scale(1)
-        permute_w4_scale()
-        stage(v2_picked, S + H, S2)
-        load_b1()
-        load_bc()
-        move_scale(nc.scalar, 0)
+        move_scale(nc.gpsimd, v2_plane, 4, v2_picked)
         round_w1(0, 0, 0, on_scalar)
         round_w1(0, 0, 1, on_scalar)
-        move_scale(nc.gpsimd, 1)
-        turn_biases()
+        bias_cols = turn_biases("w1_raw00")
         gather_v(0, 0, S)
         quantise_w1(0, 0, 0)
         quantise_w1(0, 0, 1)
-        permute_w4_codes()
         round_w1(0, 1, 0, on_scalar)
         round_w1(0, 1, 1, on_vector)
         quantise_w1(0, 1, 1)
@@ -323,12 +326,13 @@ def tile_list_ad_bid_scores_kernel(
             project_a(0, 1, h)
             project_b(0, 1, 2 * h)
             project_b(0, 1, 2 * h + 1)
-        add_b1(0, 0, P)
+        add_b1(0, 0, 1)
+        add_b1(0, 1, 1)
         round_w1(1, 0, 0, on_scalar)
         round_w1(1, 1, 0, on_scalar)
         round_w1(1, 0, 1, on_vector)
         round_w1(1, 1, 1, on_vector)
-        add_b1(0, 1, HALF, "w1_raw11")
+        add_b1(0, 2, 2, "w1_raw11")
         quantise_w1(1, 0, 1)
         quantise_w1(1, 0, 0)
         quantise_w1(1, 1, 1)
@@ -342,7 +346,11 @@ def tile_list_ad_bid_scores_kernel(
         for h in range(2):
             project_a(1, 0, h)
             project_a(1, 1, h)
-            add_b1(1, h, P if h == 0 else HALF)
+            if h == 0:
+                add_b1(1, 0, 1)
+                add_b1(1, 1, 1)
+            else:
+                add_b1(1, 2, 2)
             for c in (2 * h, 2 * h + 1):
                 project_b(1, 0, c)
                 project_b(1, 1, c)

@@ -76,8 +76,8 @@ def tile_list_ad_bid_scores_kernel(
         def load_spread(queue, plane, scales):
             queue.dma_start(out=plane[0:P:4, :], in_=scales.bitcast(I32).rearrange("a s n -> s a n"))
 
-        def move_scale(queue, plane, first, rows):
-            for q in range(4):
+        def move_scale(queue, plane, first, rows, quadrants=(0, 2, 1, 3)):
+            for q in quadrants:
                 queue.dma_start(
                     out=plane[32 * q + first : 32 * q + first + 4, :, :],
                     in_=rows[32 * q : 32 * (q + 1) : 4, :].bitcast(I32),
@@ -158,11 +158,24 @@ def tile_list_ad_bid_scores_kernel(
                 tab2_win[b][:].bitcast(U32).indirect(idx2[:, half * n // 16 : (half + 1) * n // 16]),
             )
 
-        def round_w1(b, a, u, copy):
-            w1_bf[b, a, u] = held("w1_bf%d%d%d" % (b, a, u), [P, PASS * 2], BF16)
+        def round_w1(b, a, u, copy, first=0, n=P):
+            if (b, a, u) not in w1_bf:
+                w1_bf[b, a, u] = held("w1_bf%d%d%d" % (b, a, u), [P, PASS * 2], BF16)
+            ms = slice(first, first + n)
             copy(
-                out=w1_bf[b, a, u][:].rearrange("p (t m j) -> p m j t", t=2, j=PACK),
-                in_=w1_raw[b, a].rearrange("p j (m t) -> p m j t", t=PACK)[:, :, :, 2 * u : 2 * u + 2],
+                out=w1_bf[b, a, u][:].rearrange("p (t m j) -> p m j t", t=2, j=PACK)[:, ms, :, :],
+                in_=w1_raw[b, a].rearrange("p j (m t) -> p m j t", t=PACK)[:, ms, :, 2 * u : 2 * u + 2],
+            )
+
+        def round_w1_on_gpsimd(b, a, u, first, n):
+            ms = slice(first, first + n)
+            nc.gpsimd.tensor_scalar(
+                out=w1_bf[b, a, u][:].rearrange("p (t m j) -> p t m j", t=2, j=PACK)[:, :, ms, :],
+                in0=w1_raw[b, a].rearrange("p j (m t) -> p t m j", t=PACK)[:, 2 * u : 2 * u + 2, ms, :],
+                scalar1=1.0,
+                scalar2=0.0,
+                op0=MULT,
+                op1=ADD,
             )
 
         def quantise_w1(b, a, u):
@@ -190,16 +203,16 @@ def tile_list_ad_bid_scores_kernel(
                         stop=(a == PASSES - 1 and e == 1),
                     )
 
-        def add_b1(b, c, n, tag=None):
+        def add_b1(b, c, n, tag=None, shared=False):
             sums = held("a_sb%d%d" % (b, c), [P, PACK, n * P], F32, tag)
             at = (c % 2) * P
             for t in range(PACK):
-                nc.scalar.activation(
-                    out=sums[:, t, :],
-                    in_=a_bank[b, c // 2, t // 2][:, t % 2, at : at + n * P],
-                    func=IDENTITY,
-                    bias=bias_cols[:, 0, PASSES * t + b : PASSES * t + b + 1],
-                )
+                part = a_bank[b, c // 2, t // 2][:, t % 2, at : at + n * P]
+                bias = bias_cols[:, 0, PASSES * t + b : PASSES * t + b + 1]
+                if shared and t >= 2:
+                    nc.vector.tensor_scalar(out=sums[:, t, :], in0=part, scalar1=bias, scalar2=None, op0=ADD)
+                else:
+                    nc.scalar.activation(out=sums[:, t, :], in_=part, func=IDENTITY, bias=bias)
             for e in range(n):
                 a_sb[b, c + e] = sums[:, :, e * P : (e + 1) * P]
 
@@ -219,10 +232,10 @@ def tile_list_ad_bid_scores_kernel(
                     stop=(a == PASSES - 1 and t == PACK - 1),
                 )
 
-        def interact(b, c):
+        def interact(b, c, tag=None):
             h, at = c // 2, (c % 2) * P
             if at == 0:
-                h_bf[b, h] = held("h_bf%d%d" % (b, h), [P, HALF * PACK], BF16)
+                h_bf[b, h] = held("h_bf%d%d" % (b, h), [P, HALF * PACK], BF16, tag)
             nc.vector.tensor_tensor(
                 out=h_bf[b, h][:, at * PACK : (at + P) * PACK].rearrange("p (g i t) -> p g t i", i=4, t=PACK),
                 in0=b_bank[b, c][:].rearrange("p t (g i) -> p g t i", i=4),
@@ -230,9 +243,9 @@ def tile_list_ad_bid_scores_kernel(
                 op=MULT,
             )
 
-        def quantise_h(b, h):
+        def quantise_h(b, h, tag=None):
             if h == 0:
-                h_codes[b] = held("h_codes%d" % b, [P, S], U32, None)
+                h_codes[b] = held("h_codes%d" % b, [P, S], U32, tag)
             js = slice(h * HALF, (h + 1) * HALF)
             nc.vector.quantize_mx(out=h_codes[b][:, js].bitcast(FP8X4), scales=h_scale[b][:, js], in_=h_bf[b, h][:])
 
@@ -326,22 +339,22 @@ def tile_list_ad_bid_scores_kernel(
             project_a(0, 1, h)
             project_b(0, 1, 2 * h)
             project_b(0, 1, 2 * h + 1)
-        add_b1(0, 0, 1)
-        add_b1(0, 1, 1)
+        add_b1(0, 0, 2, shared=True)
         round_w1(1, 0, 0, on_scalar)
-        round_w1(1, 1, 0, on_scalar)
-        round_w1(1, 0, 1, on_vector)
+        round_w1(1, 0, 1, on_scalar, 0, 40)
+        round_w1_on_gpsimd(1, 0, 1, 40, 88)
+        round_w1(1, 1, 0, on_vector)
         round_w1(1, 1, 1, on_vector)
-        add_b1(0, 2, 2, "w1_raw11")
-        quantise_w1(1, 0, 1)
+        add_b1(0, 2, 2, "w1_raw01")
         quantise_w1(1, 0, 0)
-        quantise_w1(1, 1, 1)
+        quantise_w1(1, 0, 1)
         quantise_w1(1, 1, 0)
+        quantise_w1(1, 1, 1)
         interact(0, 0)
         interact(0, 1)
-        quantise_h(0, 0)
-        interact(0, 2)
+        interact(0, 2, "w1_bf110")
         interact(0, 3)
+        quantise_h(0, 0, "w1_bf111")
         quantise_h(0, 1)
         for h in range(2):
             project_a(1, 0, h)
@@ -357,8 +370,8 @@ def tile_list_ad_bid_scores_kernel(
         gather_v2(0, 0)
         interact(1, 0)
         interact(1, 1)
-        interact(1, 2)
         quantise_h(1, 0)
+        interact(1, 2, "h_bf10")
         interact(1, 3)
         quantise_h(1, 1)
         for c in range(4):

@@ -23,7 +23,6 @@ PACK = 4
 PASS = P * PACK
 PASSES = 2
 HALF = S // 2
-ROW = S + H
 
 
 def tile_list_ad_bid_scores_kernel(
@@ -45,19 +44,18 @@ def tile_list_ad_bid_scores_kernel(
         idx2 = lists.tile([P, S2 // 16], U16, name="idx2")
 
         tab_plane = held("tab_plane", [P, T // 4], I32)
-        w4_plane = held("w4_plane", [P, H // 4], I32)
+        w4_plane = held("w4_plane", [P, PASSES, H // 4], I32)
         tab2_plane = held("tab2_plane", [P, T2 // 4], I32)
-        bc_rows = held("bc_rows", [P, P], F32)
-        b1_rows = held("b1_rows", [P, PASS], F32)
+        bias_rows = held("bias_rows", [P, PASS], F32)
         v2_picked = held("v2_picked", [P, S2], U8)
         w4_raw = held("w4_raw", [P, PASSES, H // 2], I32)
         w1_raw = {}
         tab_win = [held("tab_win%d" % a, [P, T], I32) for a in range(2)]
         tab2_win = [held("tab2_win%d" % a, [P, T2], I32) for a in range(2)]
+        w4_scale = held("w4_scale", [P, PASSES, H], U8, "tab_win0")
         v_picked = held("v_picked", [P, S], U8)
-        staged = held("staged", [P, ROW], U8)
         v2_plane = held("v2_plane", [P, PASSES, S2 // 4], I32)
-        planes = held("planes", [P, PASSES, ROW // 4], I32)
+        planes = held("planes", [P, PASSES, S // 4], I32)
         w1_codes = {}
         w1_scale = {(b, a): held("w1_scale%d%d" % (b, a), [P, PASS], U8) for b in range(2) for a in range(2)}
         w4_codes = held("w4_codes", [P, PASSES, 2 * H], U8)
@@ -65,7 +63,7 @@ def tile_list_ad_bid_scores_kernel(
         h_scale = [held("h_scale%d" % b, [P, S], U8) for b in range(2)]
         a_sb = {}
         h_bf = {}
-        ident = held("ident", [P, P], F32)
+        ident = held("ident", [P, P], F32, "tab_plane")
         v_codes = {}
         v2_codes = {}
         w1_bf = {}
@@ -83,8 +81,11 @@ def tile_list_ad_bid_scores_kernel(
                     in_=rows[32 * q : 32 * (q + 1) : 4, :].bitcast(I32),
                 )
 
-        def stage(picked, at, n):
-            nc.vector.tensor_copy(out=staged[:, at : at + n].bitcast(I32), in_=picked[:].bitcast(I32))
+        def load_w4_scale():
+            for r in range(4):
+                nc.gpsimd.dma_start(
+                    out=w4_plane[r:P:32, :, :], in_=w4_scales.bitcast(I32)[:, r:16:4, :].rearrange("a q n -> q a n")
+                )
 
         def load_w1(a, first, n):
             raw = held("w1_raw%d%d" % (a, first), [P, PACK, n * PASS], F32)
@@ -100,20 +101,20 @@ def tile_list_ad_bid_scores_kernel(
             nc.sync.dma_start(out=w4_raw[:], in_=w4_words.bitcast(I32).rearrange("a p n -> p a n"))
 
         def load_b1():
-            nc.sync.dma_start(out=b1_rows[0:PASSES, :], in_=b1.rearrange("(b r) -> b r", b=PASSES))
+            nc.sync.dma_start(out=bias_rows[0:PASSES, :], in_=b1.rearrange("(b r) -> b r", b=PASSES))
 
         def load_bc():
-            nc.sync.dma_start(out=bc_rows[0 : S2 // P, :], in_=bc.rearrange("(c p) -> c p", p=P))
+            nc.sync.dma_start(out=bias_rows[8:16, 0:P], in_=bc.rearrange("(c p) -> c p", p=P))
 
         def turn_biases(tag):
             both = held("bias_cols", [P, 2, PACK * PASSES], F32, tag)
             b1_bank = bank(6, [P, PACK, P])
             for t in range(PACK):
-                nc.tensor.transpose(b1_bank[:, t, :], b1_rows[:, t:PASS:PACK], ident[:])
+                nc.tensor.transpose(b1_bank[:, t, :], bias_rows[:, t:PASS:PACK], ident[:])
             nc.scalar.copy(out=both[:, 0, :].rearrange("p (t b) -> p t b", b=PASSES), in_=b1_bank[:, :, 0:PASSES])
             bc_bank = bank(7, [P, P])
-            nc.tensor.transpose(bc_bank[:], bc_rows[:], ident[:])
-            nc.scalar.copy(out=both[:, 1, :], in_=bc_bank[:, 0 : S2 // P])
+            nc.tensor.transpose(bc_bank[:], bias_rows[:, 0:P], ident[:])
+            nc.scalar.copy(out=both[:, 1, :], in_=bc_bank[:, 8:16])
             return both
 
         def permute_w4_codes():
@@ -124,8 +125,8 @@ def tile_list_ad_bid_scores_kernel(
 
         def permute_w4_scale():
             nc.vector.tensor_copy(
-                out=staged[:, S : S + H].rearrange("p (b t m) -> p b t m", b=PASSES, t=PACK),
-                in_=w4_plane[:].bitcast(U8).rearrange("p (b m t) -> p b t m", b=PASSES, t=PACK),
+                out=w4_scale[:].rearrange("p a (b t m) -> p (a b) t m", b=PASSES, t=PACK),
+                in_=w4_plane[:].bitcast(U8).rearrange("p a (b m t) -> p (a b) t m", b=PASSES, t=PACK),
             )
 
         def gather_v_scale():
@@ -143,12 +144,8 @@ def tile_list_ad_bid_scores_kernel(
             codes, at = v_codes[a, first // P]
             return codes[:, at : at + n].bitcast(FP8X4)
 
-        def gather_v2_scale(half):
-            n = S2 // 2
-            nc.vector.tensor_copy(
-                v2_picked[:, half * n : (half + 1) * n],
-                tab2_plane[:].bitcast(U8).indirect(idx2[:, half * n // 16 : (half + 1) * n // 16]),
-            )
+        def gather_v2_scale():
+            nc.vector.tensor_copy(v2_picked[:], tab2_plane[:].bitcast(U8).indirect(idx2[:]))
 
         def gather_v2(b, half):
             n = S2 // 2
@@ -165,17 +162,6 @@ def tile_list_ad_bid_scores_kernel(
             copy(
                 out=w1_bf[b, a, u][:].rearrange("p (t m j) -> p m j t", t=2, j=PACK)[:, ms, :, :],
                 in_=w1_raw[b, a].rearrange("p j (m t) -> p m j t", t=PACK)[:, ms, :, 2 * u : 2 * u + 2],
-            )
-
-        def round_w1_on_gpsimd(b, a, u, first, n):
-            ms = slice(first, first + n)
-            nc.gpsimd.tensor_scalar(
-                out=w1_bf[b, a, u][:].rearrange("p (t m j) -> p t m j", t=2, j=PACK)[:, :, ms, :],
-                in0=w1_raw[b, a].rearrange("p j (m t) -> p t m j", t=PACK)[:, 2 * u : 2 * u + 2, ms, :],
-                scalar1=1.0,
-                scalar2=0.0,
-                op0=MULT,
-                op1=ADD,
             )
 
         def quantise_w1(b, a, u):
@@ -225,7 +211,7 @@ def tile_list_ad_bid_scores_kernel(
                 nc.tensor.matmul_mx(
                     out=b_bank[b, c][:, t, :],
                     lhsT=w4_codes[:, a, 2 * col : 2 * (col + P)].bitcast(FP4X4),
-                    lhsT_scale=planes[:].bitcast(U8)[:, a, S + col : S + col + P],
+                    lhsT_scale=w4_scale[:, a, col : col + P],
                     rhs=v_cols(a, c * P, P),
                     rhs_scale=planes[:].bitcast(U8)[:, a, js],
                     start=(a == 0 and t == 0),
@@ -291,39 +277,37 @@ def tile_list_ad_bid_scores_kernel(
         nc.vector.memset(tab_plane[:], 0)
         nc.vector.memset(w4_plane[:], 0)
         nc.vector.memset(tab2_plane[:], 0)
+        nc.vector.memset(bias_rows[:, 0:HALF], 0.0)
         nc.vector.memset(planes[:], 0)
         nc.vector.memset(v2_plane[:], 0)
-        nc.vector.memset(b1_rows[:], 0.0)
-        make_identity(nc, ident[:])
         load_w4()
         nc.sync.dma_start(idx[:], offs)
         load_spread(nc.sync, tab_plane, tab_scales)
-        load_spread(nc.sync, w4_plane, w4_scales)
-        nc.scalar.copy(out=bc_rows[:], in_=ident[:])
-        load_w1(0, 0, 1)
+        load_w4_scale()
+        nc.scalar.copy(out=bias_rows[:, HALF:PASS], in_=bias_rows[:, 0:HALF])
         nc.sync.dma_start(idx2[:], offs2)
         load_spread(nc.sync, tab2_plane, tab2_scales)
+        load_w1(0, 0, 1)
         load_words(tab_win[0], tab_words[0])
         load_b1()
         load_bc()
-        load_w1(1, 0, 1)
-        permute_w4_codes()
         gather_v_scale()
-        permute_w4_scale()
-        stage(v_picked, 0, S)
-        move_scale(nc.sync, planes, 0, staged)
+        permute_w4_codes()
+        move_scale(nc.sync, planes, 0, v_picked)
+        make_identity(nc, ident[:])
+        load_w1(1, 0, 1)
         load_words(tab_win[1], tab_words[1])
         load_w1(0, 1, 1)
         load_w1(1, 1, 1)
         load_words(tab2_win[0], tab2_words[0])
         load_words(tab2_win[1], tab2_words[1])
-        gather_v2_scale(0)
-        gather_v2_scale(1)
+        gather_v2_scale()
         move_scale(nc.gpsimd, v2_plane, 4, v2_picked)
         round_w1(0, 0, 0, on_scalar)
         round_w1(0, 0, 1, on_scalar)
         bias_cols = turn_biases("w1_raw00")
         gather_v(0, 0, S)
+        permute_w4_scale()
         quantise_w1(0, 0, 0)
         quantise_w1(0, 0, 1)
         round_w1(0, 1, 0, on_scalar)
@@ -339,10 +323,11 @@ def tile_list_ad_bid_scores_kernel(
             project_a(0, 1, h)
             project_b(0, 1, 2 * h)
             project_b(0, 1, 2 * h + 1)
-        add_b1(0, 0, 2, shared=True)
+        add_b1(0, 0, 1, shared=True)
+        add_b1(0, 1, 1, shared=True)
         round_w1(1, 0, 0, on_scalar)
-        round_w1(1, 0, 1, on_scalar, 0, 40)
-        round_w1_on_gpsimd(1, 0, 1, 40, 88)
+        round_w1(1, 0, 1, on_scalar, 0, 48)
+        round_w1(1, 0, 1, on_vector, 48, 80)
         round_w1(1, 1, 0, on_vector)
         round_w1(1, 1, 1, on_vector)
         add_b1(0, 2, 2, "w1_raw01")

@@ -249,19 +249,6 @@ def tile_list_ad_bid_scores_kernel(
                 stop=not first,
             )
 
-        def warm_up(passes):
-            spare = bank(7, [P, S])
-            for n in range(passes):
-                nc.tensor.matmul_mx(
-                    out=spare[:],
-                    lhsT=w1_codes[1, 1][:, 0:P].bitcast(FP8X4),
-                    lhsT_scale=w1_scale[1, 1][:, 0:P],
-                    rhs=v_cols(0, 0, S),
-                    rhs_scale=planes[:].bitcast(U8)[:, 0, 0:S],
-                    start=True,
-                    stop=True,
-                )
-
         def store(c, on_vector):
             y_sb = held("y_sb%d" % c, [P, S], F32)
             if on_vector:
@@ -348,20 +335,20 @@ def tile_list_ad_bid_scores_kernel(
                 add_b1(1, 0, 1)
                 add_b1(1, 1, 1)
             else:
-                add_b1(1, 2, 2)
+                add_b1(1, 2, 1)
+                add_b1(1, 3, 1)
             for c in (2 * h, 2 * h + 1):
                 project_b(1, 0, c)
                 project_b(1, 1, c)
         gather_v2(0, 0)
         interact(1, 0)
         interact(1, 1)
-        quantise_h(1, 0)
-        interact(1, 2, "h_bf10")
+        interact(1, 2)
         interact(1, 3)
+        quantise_h(1, 0, "a_sb12")
         quantise_h(1, 1)
         for c in range(4):
             score(c, 0, True)
-        warm_up(2)
         gather_v2(1, 0)
         for c in range(4):
             score(c, 1, False)

@@ -108,10 +108,12 @@ def tile_list_ad_bid_scores_kernel(
 
         def turn_biases(tag):
             both = held("bias_cols", [P, 2, PACK * PASSES], F32, tag)
-            b1_bank = bank(6, [P, PACK, P])
-            for t in range(PACK):
-                nc.tensor.transpose(b1_bank[:, t, :], bias_rows[:, t:PASS:PACK], ident[:])
-            nc.scalar.copy(out=both[:, 0, :].rearrange("p (t b) -> p t b", b=PASSES), in_=b1_bank[:, :, 0:PASSES])
+            b1_cols = both[:, 0, :].rearrange("p (t b) -> p t b", b=PASSES)
+            for u in range(2):
+                b1_bank = bank(2 + u, [P, 2, P])
+                for e in range(2):
+                    nc.tensor.transpose(b1_bank[:, e, :], bias_rows[:, 2 * u + e : PASS : PACK], ident[:])
+                nc.scalar.copy(out=b1_cols[:, 2 * u : 2 * u + 2, :], in_=b1_bank[:, :, 0:PASSES])
             bc_bank = bank(7, [P, P])
             nc.tensor.transpose(bc_bank[:], bias_rows[:, 0:P], ident[:])
             nc.scalar.copy(out=both[:, 1, :], in_=bc_bank[:, 8:16])
@@ -292,13 +294,13 @@ def tile_list_ad_bid_scores_kernel(
         move_scale(nc.gpsimd, v2_plane, 4, v2_picked)
         round_w1(0, 0, 0, on_scalar)
         round_w1(0, 0, 1, on_scalar)
-        bias_cols = turn_biases("w1_raw00")
         gather_v(0, 0, S)
         permute_w4_scale()
         quantise_w1(0, 0, 0)
         quantise_w1(0, 0, 1)
         round_w1(0, 1, 0, on_scalar)
         round_w1(0, 1, 1, on_vector)
+        bias_cols = turn_biases("w1_raw10")
         quantise_w1(0, 1, 1)
         quantise_w1(0, 1, 0)
         for h in range(2):
@@ -349,6 +351,16 @@ def tile_list_ad_bid_scores_kernel(
         quantise_h(1, 1)
         for c in range(4):
             score(c, 0, True)
+        for c in range(4, 6):
+            nc.tensor.matmul_mx(
+                out=bank(c, [P, S])[:],
+                lhsT=v2_codes[0, 0][:, 0:P].bitcast(FP8X4),
+                lhsT_scale=v2_plane[:].bitcast(U8)[4:P, 0, 0:P],
+                rhs=h_codes[1][:].bitcast(FP8X4),
+                rhs_scale=h_scale[1][:],
+                start=True,
+                stop=True,
+            )
         gather_v2(1, 0)
         for c in range(4):
             score(c, 1, False)
@@ -356,6 +368,7 @@ def tile_list_ad_bid_scores_kernel(
         gather_v2(0, 1)
         for c in range(4, 8):
             score(c, 1, True)
+        for c in range(4, 8):
             score(c, 0, False)
         for c in range(8):
             store(c, c in (5, 7))

@@ -151,7 +151,7 @@ def tile_list_ad_bid_scores_kernel(
 
         def gather_v2(b, half):
             n = S2 // 2
-            v2_codes[b, half] = held("v2_codes%d%d" % (b, half), [P, n], U32, "tab2_win1" if (b, half) == (0, 1) else None)
+            v2_codes[b, half] = held("v2_codes%d%d" % (b, half), [P, n], U32)
             nc.vector.tensor_copy(
                 v2_codes[b, half][:],
                 tab2_win[b][:].bitcast(U32).indirect(idx2[:, half * n // 16 : (half + 1) * n // 16]),
@@ -251,15 +251,16 @@ def tile_list_ad_bid_scores_kernel(
                 stop=not first,
             )
 
-        def store(c, on_vector):
-            y_sb = held("y_sb%d" % c, [P, S], F32)
-            if on_vector:
-                nc.vector.tensor_scalar(
-                    out=y_sb[:], in0=y_bank[c][:], scalar1=bias_cols[:, 1, c : c + 1], scalar2=None, op0=ADD
-                )
-            else:
-                nc.scalar.activation(out=y_sb[:], in_=y_bank[c][:], func=IDENTITY, bias=bias_cols[:, 1, c : c + 1])
-            nc.sync.dma_start(out=out[c * P : (c + 1) * P, :], in_=y_sb[:])
+        def store(blocks):
+            y_sb = held("y_sb%d" % blocks[0], [P, len(blocks), S], F32)
+            for e, c in enumerate(blocks):
+                bias = bias_cols[:, 1, c : c + 1]
+                if c in (2, 4, 6):
+                    nc.vector.tensor_scalar(out=y_sb[:, e, :], in0=y_bank[c][:], scalar1=bias, scalar2=None, op0=ADD)
+                else:
+                    nc.scalar.activation(out=y_sb[:, e, :], in_=y_bank[c][:], func=IDENTITY, bias=bias)
+            rows = out[blocks[0] * P : (blocks[-1] + 1) * P, :]
+            nc.sync.dma_start(out=rows.rearrange("(e p) j -> p e j", p=P), in_=y_sb[:])
 
         on_scalar, on_vector = nc.scalar.copy, nc.vector.tensor_copy
 
@@ -343,32 +344,18 @@ def tile_list_ad_bid_scores_kernel(
                 project_b(1, 0, c)
                 project_b(1, 1, c)
         gather_v2(0, 0)
+        gather_v2(0, 1)
         interact(1, 0)
         interact(1, 1)
         interact(1, 2)
         interact(1, 3)
         quantise_h(1, 0, "a_sb12")
         quantise_h(1, 1)
-        for c in range(4):
-            score(c, 0, True)
-        for c in range(4, 6):
-            nc.tensor.matmul_mx(
-                out=bank(c, [P, S])[:],
-                lhsT=v2_codes[0, 0][:, 0:P].bitcast(FP8X4),
-                lhsT_scale=v2_plane[:].bitcast(U8)[4:P, 0, 0:P],
-                rhs=h_codes[1][:].bitcast(FP8X4),
-                rhs_scale=h_scale[1][:],
-                start=True,
-                stop=True,
-            )
-        gather_v2(1, 0)
-        for c in range(4):
-            score(c, 1, False)
-        gather_v2(1, 1)
-        gather_v2(0, 1)
-        for c in range(4, 8):
-            score(c, 1, True)
-        for c in range(4, 8):
-            score(c, 0, False)
         for c in range(8):
-            store(c, c in (5, 7))
+            score(c, 0, True)
+        for half in range(2):
+            gather_v2(1, half)
+            for c in range(4 * half, 4 * half + 4):
+                score(c, 1, False)
+        for blocks in ((0,), (1, 2), (3, 4), (5, 6, 7)):
+            store(blocks)

@@ -101,7 +101,7 @@ def tile_list_ad_bid_scores_kernel(
             nc.sync.dma_start(out=w4_raw[:], in_=w4_words.bitcast(I32).rearrange("a p n -> p a n"))
 
         def load_b1():
-            nc.sync.dma_start(out=bias_rows[0:PASSES, :], in_=b1.rearrange("(b r) -> b r", b=PASSES))
+            nc.sync.dma_start(out=bias_rows[16:P:64, :], in_=b1.rearrange("(b r) -> b r", b=PASSES))
 
         def load_bc():
             nc.sync.dma_start(out=bias_rows[8:16, 0:P], in_=bc.rearrange("(c p) -> c p", p=P))
@@ -113,7 +113,7 @@ def tile_list_ad_bid_scores_kernel(
                 b1_bank = bank(2 + u, [P, 2, P])
                 for e in range(2):
                     nc.tensor.transpose(b1_bank[:, e, :], bias_rows[:, 2 * u + e : PASS : PACK], ident[:])
-                nc.scalar.copy(out=b1_cols[:, 2 * u : 2 * u + 2, :], in_=b1_bank[:, :, 0:PASSES])
+                nc.scalar.copy(out=b1_cols[:, 2 * u : 2 * u + 2, :], in_=b1_bank[:, :, 16:P:64])
             bc_bank = bank(7, [P, P])
             nc.tensor.transpose(bc_bank[:], bias_rows[:, 0:P], ident[:])
             nc.scalar.copy(out=both[:, 1, :], in_=bc_bank[:, 8:16])
@@ -151,7 +151,7 @@ def tile_list_ad_bid_scores_kernel(
 
         def gather_v2(b, half):
             n = S2 // 2
-            v2_codes[b, half] = held("v2_codes%d%d" % (b, half), [P, n], U32)
+            v2_codes[b, half] = held("v2_codes%d%d" % (b, half), [P, n], U32, "a_sb13" if (b, half) == (0, 1) else None)
             nc.vector.tensor_copy(
                 v2_codes[b, half][:],
                 tab2_win[b][:].bitcast(U32).indirect(idx2[:, half * n // 16 : (half + 1) * n // 16]),
@@ -237,29 +237,30 @@ def tile_list_ad_bid_scores_kernel(
             js = slice(h * HALF, (h + 1) * HALF)
             nc.vector.quantize_mx(out=h_codes[b][:, js].bitcast(FP8X4), scales=h_scale[b][:, js], in_=h_bf[b, h][:])
 
-        def score(c, b, first):
-            if first:
-                y_bank[c] = bank(c, [P, S])
+        def score(c, b, js=slice(0, S), index=None):
+            if b == 0:
+                y_bank[c, js.start] = bank(c if index is None else index, [P, js.stop - js.start])
             cols = slice((c % 4) * P, (c % 4 + 1) * P)
             nc.tensor.matmul_mx(
-                out=y_bank[c][:],
+                out=y_bank[c, js.start][:],
                 lhsT=v2_codes[b, c // 4][:, cols].bitcast(FP8X4),
                 lhsT_scale=v2_plane[:].bitcast(U8)[4:P, b, c * P : (c + 1) * P],
-                rhs=h_codes[b][:].bitcast(FP8X4),
-                rhs_scale=h_scale[b][:],
-                start=first,
-                stop=not first,
+                rhs=h_codes[b][:, js].bitcast(FP8X4),
+                rhs_scale=h_scale[b][:, js],
+                start=(b == 0),
+                stop=(b == 1),
             )
 
-        def store(blocks):
-            y_sb = held("y_sb%d" % blocks[0], [P, len(blocks), S], F32)
+        def add_bc(blocks, js=slice(0, S)):
+            y_sb = held("y_sb%d_%d" % (blocks[0], js.start), [P, len(blocks), js.stop - js.start], F32)
             for e, c in enumerate(blocks):
                 bias = bias_cols[:, 1, c : c + 1]
-                if c in (2, 4, 6):
-                    nc.vector.tensor_scalar(out=y_sb[:, e, :], in0=y_bank[c][:], scalar1=bias, scalar2=None, op0=ADD)
+                sums = y_bank[c, js.start][:]
+                if c in (3, 4, 6):
+                    nc.vector.tensor_scalar(out=y_sb[:, e, :], in0=sums, scalar1=bias, scalar2=None, op0=ADD)
                 else:
-                    nc.scalar.activation(out=y_sb[:, e, :], in_=y_bank[c][:], func=IDENTITY, bias=bias)
-            rows = out[blocks[0] * P : (blocks[-1] + 1) * P, :]
+                    nc.scalar.activation(out=y_sb[:, e, :], in_=sums, func=IDENTITY, bias=bias)
+            rows = out[blocks[0] * P : (blocks[-1] + 1) * P, js]
             nc.sync.dma_start(out=rows.rearrange("(e p) j -> p e j", p=P), in_=y_sb[:])
 
         on_scalar, on_vector = nc.scalar.copy, nc.vector.tensor_copy
@@ -344,18 +345,29 @@ def tile_list_ad_bid_scores_kernel(
                 project_b(1, 0, c)
                 project_b(1, 1, c)
         gather_v2(0, 0)
-        gather_v2(0, 1)
         interact(1, 0)
         interact(1, 1)
         interact(1, 2)
         interact(1, 3)
         quantise_h(1, 0, "a_sb12")
+        gather_v2(0, 1)
         quantise_h(1, 1)
-        for c in range(8):
-            score(c, 0, True)
-        for half in range(2):
-            gather_v2(1, half)
-            for c in range(4 * half, 4 * half + 4):
-                score(c, 1, False)
-        for blocks in ((0,), (1, 2), (3, 4), (5, 6, 7)):
-            store(blocks)
+        halves = [slice(0, HALF), slice(HALF, S)]
+        score(0, 0, halves[0])
+        for c in range(1, 7):
+            score(c, 0)
+        score(0, 0, halves[1], 7)
+        gather_v2(1, 0)
+        for js in halves:
+            score(0, 1, js)
+        for c in range(1, 4):
+            score(c, 1)
+        gather_v2(1, 1)
+        for js in halves:
+            add_bc((0,), js)
+        for c in range(4, 7):
+            score(c, 1)
+        score(7, 0, index=0)
+        score(7, 1)
+        for blocks in ((1,), (2, 3), (4, 5, 6, 7)):
+            add_bc(blocks)

@@ -149,13 +149,13 @@ def tile_list_ad_bid_scores_kernel(
         def gather_v2_scale():
             nc.vector.tensor_copy(v2_picked[:], tab2_plane[:].bitcast(U8).indirect(idx2[:]))
 
-        def gather_v2(b, half):
-            n = S2 // 2
-            v2_codes[b, half] = held("v2_codes%d%d" % (b, half), [P, n], U32, "a_sb13" if (b, half) == (0, 1) else None)
+        def gather_v2(b, first, n, tag=None):
+            codes = held("v2_codes%d_%d" % (b, first), [P, n], U32, tag)
             nc.vector.tensor_copy(
-                v2_codes[b, half][:],
-                tab2_win[b][:].bitcast(U32).indirect(idx2[:, half * n // 16 : (half + 1) * n // 16]),
+                codes[:], tab2_win[b][:].bitcast(U32).indirect(idx2[:, first // 16 : (first + n) // 16])
             )
+            for c in range(first // P, (first + n) // P):
+                v2_codes[b, c] = codes[:, c * P - first : (c + 1) * P - first]
 
         def round_w1(b, a, u, copy, first=0, n=P):
             if (b, a, u) not in w1_bf:
@@ -237,30 +237,29 @@ def tile_list_ad_bid_scores_kernel(
             js = slice(h * HALF, (h + 1) * HALF)
             nc.vector.quantize_mx(out=h_codes[b][:, js].bitcast(FP8X4), scales=h_scale[b][:, js], in_=h_bf[b, h][:])
 
-        def score(c, b, js=slice(0, S), index=None):
+        def score(c, b):
             if b == 0:
-                y_bank[c, js.start] = bank(c if index is None else index, [P, js.stop - js.start])
-            cols = slice((c % 4) * P, (c % 4 + 1) * P)
+                y_bank[c] = bank(c, [P, S])
             nc.tensor.matmul_mx(
-                out=y_bank[c, js.start][:],
-                lhsT=v2_codes[b, c // 4][:, cols].bitcast(FP8X4),
+                out=y_bank[c][:],
+                lhsT=v2_codes[b, c].bitcast(FP8X4),
                 lhsT_scale=v2_plane[:].bitcast(U8)[4:P, b, c * P : (c + 1) * P],
-                rhs=h_codes[b][:, js].bitcast(FP8X4),
-                rhs_scale=h_scale[b][:, js],
+                rhs=h_codes[b][:].bitcast(FP8X4),
+                rhs_scale=h_scale[b][:],
                 start=(b == 0),
                 stop=(b == 1),
             )
 
-        def add_bc(blocks, js=slice(0, S)):
-            y_sb = held("y_sb%d_%d" % (blocks[0], js.start), [P, len(blocks), js.stop - js.start], F32)
+        def add_bc(blocks):
+            y_sb = held("y_sb%d" % blocks[0], [P, len(blocks), S], F32)
             for e, c in enumerate(blocks):
                 bias = bias_cols[:, 1, c : c + 1]
-                sums = y_bank[c, js.start][:]
-                if c in (3, 4, 6):
+                sums = y_bank[c][:]
+                if c in (3, 5, 7):
                     nc.vector.tensor_scalar(out=y_sb[:, e, :], in0=sums, scalar1=bias, scalar2=None, op0=ADD)
                 else:
                     nc.scalar.activation(out=y_sb[:, e, :], in_=sums, func=IDENTITY, bias=bias)
-            rows = out[blocks[0] * P : (blocks[-1] + 1) * P, js]
+            rows = out[blocks[0] * P : (blocks[-1] + 1) * P, :]
             nc.sync.dma_start(out=rows.rearrange("(e p) j -> p e j", p=P), in_=y_sb[:])
 
         on_scalar, on_vector = nc.scalar.copy, nc.vector.tensor_copy
@@ -344,30 +343,19 @@ def tile_list_ad_bid_scores_kernel(
             for c in (2 * h, 2 * h + 1):
                 project_b(1, 0, c)
                 project_b(1, 1, c)
-        gather_v2(0, 0)
+        gather_v2(0, 0, PASS)
         interact(1, 0)
         interact(1, 1)
         interact(1, 2)
         interact(1, 3)
         quantise_h(1, 0, "a_sb12")
-        gather_v2(0, 1)
+        gather_v2(0, PASS, PASS, "a_sb13")
         quantise_h(1, 1)
-        halves = [slice(0, HALF), slice(HALF, S)]
-        score(0, 0, halves[0])
-        for c in range(1, 7):
+        for c in range(8):
             score(c, 0)
-        score(0, 0, halves[1], 7)
-        gather_v2(1, 0)
-        for js in halves:
-            score(0, 1, js)
-        for c in range(1, 4):
-            score(c, 1)
-        gather_v2(1, 1)
-        for js in halves:
-            add_bc((0,), js)
-        for c in range(4, 7):
-            score(c, 1)
-        score(7, 0, index=0)
-        score(7, 1)
-        for blocks in ((1,), (2, 3), (4, 5, 6, 7)):
+        for pair in range(4):
+            gather_v2(1, pair * 2 * P, 2 * P)
+            score(2 * pair, 1)
+            score(2 * pair + 1, 1)
+        for blocks in ((0,), (1,), (2,), (3, 4), (5, 6, 7)):
             add_bc(blocks)

from contextlib import ExitStack

import concourse.mybir as mybir
from concourse.masks import make_identity

K, T, S, H, T2, S2 = 1024, 2048, 512, 1024, 4096, 1024
FLOPS = 2 * (2 * K * H * S + H * S2 * S)

F32 = mybir.dt.float32
BF16 = mybir.dt.bfloat16
I32 = mybir.dt.int32
U32 = mybir.dt.uint32
U16 = mybir.dt.uint16
U8 = mybir.dt.uint8
FP8X4 = mybir.dt.float8_e4m3fn_x4
FP4X4 = mybir.dt.float4_e2m1fn_x4
IDENTITY = mybir.ActivationFunctionType.Identity
MULT = mybir.AluOpType.mult
ADD = mybir.AluOpType.add

P = 128
PACK = 4
PASS = P * PACK
PASSES = 2
HALF = S // 2


def tile_list_ad_bid_scores_kernel(
    tc, tab_words, tab_scales, offs, tab2_words, tab2_scales, offs2, w1, b1, w4_words, w4_scales, bc, out
):
    nc = tc.nc
    with ExitStack() as ctx:
        lists = ctx.enter_context(tc.tile_pool(name="lists", bufs=1))
        keep = ctx.enter_context(tc.tile_pool(name="keep", bufs=1))
        psum = ctx.enter_context(tc.psum_pool(name="psum", bufs=1))

        def held(name, shape, dtype, tag=None):
            return keep.tile(shape, dtype, name=name, tag=tag or name, align_bytes=64)

        def bank(index, shape):
            return psum.tile(shape, F32, name="bank%d" % index, tag="bank%d" % index)

        idx = lists.tile([P, S // 16], U16, name="idx")
        idx2 = lists.tile([P, S2 // 16], U16, name="idx2")

        tab_plane = held("tab_plane", [P, T // 4], I32)
        w4_plane = held("w4_plane", [P, PASSES, H // 4], I32)
        tab2_plane = held("tab2_plane", [P, T2 // 4], I32)
        bias_rows = held("bias_rows", [P, PASS], F32)
        v2_picked = held("v2_picked", [P, S2], U8)
        w4_raw = held("w4_raw", [P, PASSES, H // 2], I32)
        w1_raw = {}
        tab_win = [held("tab_win%d" % a, [P, T], I32) for a in range(2)]
        tab2_win = [held("tab2_win%d" % a, [P, T2], I32) for a in range(2)]
        w4_scale = held("w4_scale", [P, PASSES, H], U8, "tab_win0")
        v_picked = held("v_picked", [P, S], U8)
        v2_plane = held("v2_plane", [P, PASSES, S2 // 4], I32)
        planes = held("planes", [P, PASSES, S // 4], I32)
        w1_codes = {}
        w1_scale = {(b, a): held("w1_scale%d%d" % (b, a), [P, PASS], U8) for b in range(2) for a in range(2)}
        w4_codes = held("w4_codes", [P, PASSES, 2 * H], U8)
        h_codes = {}
        h_scale = [held("h_scale%d" % b, [P, S], U8) for b in range(2)]
        a_sb = {}
        h_bf = {}
        ident = held("ident", [P, P], F32, "tab_plane")
        v_codes = {}
        v2_codes = {}
        w1_bf = {}
        a_bank = {}
        b_bank = {}
        y_bank = {}

        def load_spread(queue, plane, scales):
            queue.dma_start(out=plane[0:P:4, :], in_=scales.bitcast(I32).rearrange("a s n -> s a n"))

        def move_scale(queue, plane, first, rows, quadrants=(0, 2, 1, 3)):
            for q in quadrants:
                queue.dma_start(
                    out=plane[32 * q + first : 32 * q + first + 4, :, :],
                    in_=rows[32 * q : 32 * (q + 1) : 4, :].bitcast(I32),
                )

        def load_w4_scale():
            for r in range(4):
                nc.gpsimd.dma_start(
                    out=w4_plane[r:P:32, :, :], in_=w4_scales.bitcast(I32)[:, r:16:4, :].rearrange("a q n -> q a n")
                )

        def load_w1(a, first, n):
            raw = held("w1_raw%d%d" % (a, first), [P, PACK, n * PASS], F32)
            rows = w1[a * PASS : (a + 1) * PASS, first * PASS : (first + n) * PASS]
            nc.sync.dma_start(out=raw[:], in_=rows.rearrange("(p j) c -> p j c", j=PACK))
            for b in range(first, first + n):
                w1_raw[b, a] = raw[:, :, (b - first) * PASS : (b - first + 1) * PASS]

        def load_words(win, words):
            nc.sync.dma_start(out=win[:], in_=words.rearrange("p t i -> p (t i)").bitcast(I32))

        def load_w4():
            nc.sync.dma_start(out=w4_raw[:], in_=w4_words.bitcast(I32).rearrange("a p n -> p a n"))

        def load_b1():
            nc.sync.dma_start(out=bias_rows[16:P:64, :], in_=b1.rearrange("(b r) -> b r", b=PASSES))

        def load_bc():
            nc.sync.dma_start(out=bias_rows[8:16, 0:P], in_=bc.rearrange("(c p) -> c p", p=P))

        def turn_biases(tag):
            both = held("bias_cols", [P, 2, PACK * PASSES], F32, tag)
            b1_cols = both[:, 0, :].rearrange("p (t b) -> p t b", b=PASSES)
            for u in range(2):
                b1_bank = bank(2 + u, [P, 2, P])
                for e in range(2):
                    nc.tensor.transpose(b1_bank[:, e, :], bias_rows[:, 2 * u + e : PASS : PACK], ident[:])
                nc.scalar.copy(out=b1_cols[:, 2 * u : 2 * u + 2, :], in_=b1_bank[:, :, 16:P:64])
            bc_bank = bank(7, [P, P])
            nc.tensor.transpose(bc_bank[:], bias_rows[:, 0:P], ident[:])
            nc.scalar.copy(out=both[:, 1, :], in_=bc_bank[:, 8:16])
            return both

        def permute_w4_codes():
            nc.vector.tensor_copy(
                out=w4_codes[:].bitcast(U16).rearrange("p a (b t m) -> p (a b) t m", b=PASSES, t=PACK),
                in_=w4_raw[:].bitcast(U16).rearrange("p a (b m t) -> p (a b) t m", b=PASSES, t=PACK),
            )

        def permute_w4_scale():
            nc.vector.tensor_copy(
                out=w4_scale[:].rearrange("p a (b t m) -> p (a b) t m", b=PASSES, t=PACK),
                in_=w4_plane[:].bitcast(U8).rearrange("p a (b m t) -> p (a b) t m", b=PASSES, t=PACK),
            )

        def gather_v_scale():
            nc.vector.tensor_copy(v_picked[:], tab_plane[:].bitcast(U8).indirect(idx[:]))

        def gather_v(a, first, n):
            codes = held("v_codes%d_%d" % (a, first), [P, n], U32)
            nc.vector.tensor_copy(
                codes[:], tab_win[a][:].bitcast(U32).indirect(idx[:, first // 16 : (first + n) // 16])
            )
            for c in range(first // P, (first + n) // P):
                v_codes[a, c] = (codes, c * P - first)

        def v_cols(a, first, n):
            codes, at = v_codes[a, first // P]
            return codes[:, at : at + n].bitcast(FP8X4)

        def gather_v2_scale():
            nc.vector.tensor_copy(v2_picked[:], tab2_plane[:].bitcast(U8).indirect(idx2[:]))

        def gather_v2(b, first, n, tag=None):
            codes = held("v2_codes%d_%d" % (b, first), [P, n], U32, tag)
            nc.vector.tensor_copy(
                codes[:], tab2_win[b][:].bitcast(U32).indirect(idx2[:, first // 16 : (first + n) // 16])
            )
            for c in range(first // P, (first + n) // P):
                v2_codes[b, c] = codes[:, c * P - first : (c + 1) * P - first]

        def round_w1(b, a, u, copy, first=0, n=P):
            if (b, a, u) not in w1_bf:
                w1_bf[b, a, u] = held("w1_bf%d%d%d" % (b, a, u), [P, PASS * 2], BF16)
            ms = slice(first, first + n)
            copy(
                out=w1_bf[b, a, u][:].rearrange("p (t m j) -> p m j t", t=2, j=PACK)[:, ms, :, :],
                in_=w1_raw[b, a].rearrange("p j (m t) -> p m j t", t=PACK)[:, ms, :, 2 * u : 2 * u + 2],
            )

        def quantise_w1(b, a, u):
            if (b, a) not in w1_codes:
                w1_codes[b, a] = held("w1_codes%d%d" % (b, a), [P, PASS], U32)
            cols = slice(2 * u * P, 2 * (u + 1) * P)
            nc.vector.quantize_mx(
                out=w1_codes[b, a][:, cols].bitcast(FP8X4), scales=w1_scale[b, a][:, cols], in_=w1_bf[b, a, u][:]
            )

        def project_a(b, a, h):
            js = slice(h * HALF, (h + 1) * HALF)
            for u in range(2):
                if a == 0:
                    a_bank[b, h, u] = bank(2 * h + u, [P, 2, HALF])
                for e in range(2):
                    cols = slice((2 * u + e) * P, (2 * u + e + 1) * P)
                    nc.tensor.matmul_mx(
                        out=a_bank[b, h, u][:, e, :],
                        lhsT=w1_codes[b, a][:, cols].bitcast(FP8X4),
                        lhsT_scale=w1_scale[b, a][:, cols],
                        rhs=v_cols(a, h * HALF, HALF),
                        rhs_scale=planes[:].bitcast(U8)[:, a, js],
                        start=(a == 0 and e == 0),
                        stop=(a == PASSES - 1 and e == 1),
                    )

        def add_b1(b, c, n, tag=None, shared=False):
            sums = held("a_sb%d%d" % (b, c), [P, PACK, n * P], F32, tag)
            at = (c % 2) * P
            for t in range(PACK):
                part = a_bank[b, c // 2, t // 2][:, t % 2, at : at + n * P]
                bias = bias_cols[:, 0, PASSES * t + b : PASSES * t + b + 1]
                if shared and t >= 2:
                    nc.vector.tensor_scalar(out=sums[:, t, :], in0=part, scalar1=bias, scalar2=None, op0=ADD)
                else:
                    nc.scalar.activation(out=sums[:, t, :], in_=part, func=IDENTITY, bias=bias)
            for e in range(n):
                a_sb[b, c + e] = sums[:, :, e * P : (e + 1) * P]

        def project_b(b, a, c):
            if a == 0:
                b_bank[b, c] = bank(PACK + c, [P, PACK, P])
            js = slice(c * P, (c + 1) * P)
            for t in range(PACK):
                col = b * PASS + t * P
                nc.tensor.matmul_mx(
                    out=b_bank[b, c][:, t, :],
                    lhsT=w4_codes[:, a, 2 * col : 2 * (col + P)].bitcast(FP4X4),
                    lhsT_scale=w4_scale[:, a, col : col + P],
                    rhs=v_cols(a, c * P, P),
                    rhs_scale=planes[:].bitcast(U8)[:, a, js],
                    start=(a == 0 and t == 0),
                    stop=(a == PASSES - 1 and t == PACK - 1),
                )

        def interact(b, c, tag=None):
            h, at = c // 2, (c % 2) * P
            if at == 0:
                h_bf[b, h] = held("h_bf%d%d" % (b, h), [P, HALF * PACK], BF16, tag)
            nc.vector.tensor_tensor(
                out=h_bf[b, h][:, at * PACK : (at + P) * PACK].rearrange("p (g i t) -> p g t i", i=4, t=PACK),
                in0=b_bank[b, c][:].rearrange("p t (g i) -> p g t i", i=4),
                in1=a_sb[b, c].rearrange("p t (g i) -> p g t i", i=4),
                op=MULT,
            )

        def quantise_h(b, h, tag=None):
            if h == 0:
                h_codes[b] = held("h_codes%d" % b, [P, S], U32, tag)
            js = slice(h * HALF, (h + 1) * HALF)
            nc.vector.quantize_mx(out=h_codes[b][:, js].bitcast(FP8X4), scales=h_scale[b][:, js], in_=h_bf[b, h][:])

        def score(c, b):
            if b == 0:
                y_bank[c] = bank(c, [P, S])
            nc.tensor.matmul_mx(
                out=y_bank[c][:],
                lhsT=v2_codes[b, c].bitcast(FP8X4),
                lhsT_scale=v2_plane[:].bitcast(U8)[4:P, b, c * P : (c + 1) * P],
                rhs=h_codes[b][:].bitcast(FP8X4),
                rhs_scale=h_scale[b][:],
                start=(b == 0),
                stop=(b == 1),
            )

        def add_bc(blocks):
            y_sb = held("y_sb%d" % blocks[0], [P, len(blocks), S], F32)
            for e, c in enumerate(blocks):
                bias = bias_cols[:, 1, c : c + 1]
                sums = y_bank[c][:]
                if c in (3, 5, 7):
                    nc.vector.tensor_scalar(out=y_sb[:, e, :], in0=sums, scalar1=bias, scalar2=None, op0=ADD)
                else:
                    nc.scalar.activation(out=y_sb[:, e, :], in_=sums, func=IDENTITY, bias=bias)
            rows = out[blocks[0] * P : (blocks[-1] + 1) * P, :]
            nc.sync.dma_start(out=rows.rearrange("(e p) j -> p e j", p=P), in_=y_sb[:])

        on_scalar, on_vector = nc.scalar.copy, nc.vector.tensor_copy

        nc.vector.memset(tab_plane[:], 0)
        nc.vector.memset(w4_plane[:], 0)
        nc.vector.memset(tab2_plane[:], 0)
        nc.vector.memset(bias_rows[:, 0:HALF], 0.0)
        nc.vector.memset(planes[:], 0)
        nc.vector.memset(v2_plane[:], 0)
        load_w4()
        nc.sync.dma_start(idx[:], offs)
        load_spread(nc.sync, tab_plane, tab_scales)
        load_w4_scale()
        nc.scalar.copy(out=bias_rows[:, HALF:PASS], in_=bias_rows[:, 0:HALF])
        nc.sync.dma_start(idx2[:], offs2)
        load_spread(nc.sync, tab2_plane, tab2_scales)
        load_w1(0, 0, 1)
        load_words(tab_win[0], tab_words[0])
        load_b1()
        load_bc()
        gather_v_scale()
        permute_w4_codes()
        move_scale(nc.sync, planes, 0, v_picked)
        make_identity(nc, ident[:])
        load_w1(1, 0, 1)
        load_words(tab_win[1], tab_words[1])
        load_w1(0, 1, 1)
        load_w1(1, 1, 1)
        load_words(tab2_win[0], tab2_words[0])
        load_words(tab2_win[1], tab2_words[1])
        gather_v2_scale()
        move_scale(nc.gpsimd, v2_plane, 4, v2_picked)
        round_w1(0, 0, 0, on_scalar)
        round_w1(0, 0, 1, on_scalar)
        gather_v(0, 0, S)
        permute_w4_scale()
        quantise_w1(0, 0, 0)
        quantise_w1(0, 0, 1)
        round_w1(0, 1, 0, on_scalar)
        round_w1(0, 1, 1, on_vector)
        bias_cols = turn_biases("w1_raw10")
        quantise_w1(0, 1, 1)
        quantise_w1(0, 1, 0)
        for h in range(2):
            project_a(0, 0, h)
        for c in range(4):
            project_b(0, 0, c)
        for h in range(2):
            gather_v(1, h * HALF, HALF)
            project_a(0, 1, h)
            project_b(0, 1, 2 * h)
            project_b(0, 1, 2 * h + 1)
        add_b1(0, 0, 1, shared=True)
        add_b1(0, 1, 1, shared=True)
        round_w1(1, 0, 0, on_scalar)
        round_w1(1, 0, 1, on_scalar, 0, 48)
        round_w1(1, 0, 1, on_vector, 48, 80)
        round_w1(1, 1, 0, on_vector)
        round_w1(1, 1, 1, on_vector)
        add_b1(0, 2, 2, "w1_raw01")
        quantise_w1(1, 0, 0)
        quantise_w1(1, 0, 1)
        quantise_w1(1, 1, 0)
        quantise_w1(1, 1, 1)
        interact(0, 0)
        interact(0, 1)
        interact(0, 2, "w1_bf110")
        interact(0, 3)
        quantise_h(0, 0, "w1_bf111")
        quantise_h(0, 1)
        for h in range(2):
            project_a(1, 0, h)
            project_a(1, 1, h)
            if h == 0:
                add_b1(1, 0, 1)
                add_b1(1, 1, 1)
            else:
                add_b1(1, 2, 1)
                add_b1(1, 3, 1)
            for c in (2 * h, 2 * h + 1):
                project_b(1, 0, c)
                project_b(1, 1, c)
        gather_v2(0, 0, PASS)
        interact(1, 0)
        interact(1, 1)
        interact(1, 2)
        interact(1, 3)
        quantise_h(1, 0, "a_sb12")
        gather_v2(0, PASS, PASS, "a_sb13")
        quantise_h(1, 1)
        for c in range(8):
            score(c, 0)
        for pair in range(4):
            gather_v2(1, pair * 2 * P, 2 * P)
            score(2 * pair, 1)
            score(2 * pair + 1, 1)
        for blocks in ((0,), (1,), (2,), (3, 4), (5, 6, 7)):
            add_bc(blocks)
